import numpy as np
import ml_dtypes


def mxq(x, axis, fmt="e4m3"):
    dtype, down = {"e4m3": (ml_dtypes.float8_e4m3fn, 7), "e5m2": (ml_dtypes.float8_e5m2, 14)}[fmt]
    v = np.moveaxis(np.asarray(x, np.float32).astype(ml_dtypes.bfloat16).astype(np.float64), axis, -1)
    blocks = v.reshape(v.shape[:-1] + (-1, 32))
    amax = np.abs(blocks).max(-1, keepdims=True)
    byte = np.maximum(np.where(amax > 0, np.frexp(amax)[1] - 1 + 127, 0) - down, 1)
    scale = np.exp2(byte - 127.0)
    codes = (blocks / scale).astype(np.float32).astype(dtype).astype(np.float64)
    return np.moveaxis((codes * scale).reshape(v.shape), -1, axis)


WIDE = False


def mx_kscale(k):
    if not WIDE:
        return np.ones(k)
    levels = np.array([10, -10, 5, -5, 0])
    if k % 512:
        return np.exp2(np.random.permutation(np.resize(levels, k // 32))).repeat(32)
    a = np.empty((k // 512, 16))
    for p in range(k // 512):
        a[p, :8] = np.random.permutation(np.resize(levels, 8))
        for g in range(8):
            far = levels[np.abs(levels - a[p, g]) >= 10]
            a[p, g + 8] = far[np.random.randint(len(far))]
    return np.exp2(a.ravel()).repeat(32)


def f64(x):
    return np.asarray(x).astype(np.float64)


def striped(idx):
    return np.tile(idx.reshape(-1, 16).T, (8, 1)).astype(np.uint16)


def unstriped(offs):
    return offs[:16].T.reshape(-1).astype(np.int64)


def pack_weight(w):
    k, n = w.shape
    w = f64(np.asarray(w, np.float32).astype(ml_dtypes.bfloat16)).reshape(k // 32, 32, n)
    amax = np.abs(w).max(1)
    byte = np.clip(np.where(amax > 0, np.frexp(amax)[1] - 1 + 127 - 7, 1), 1, 254)
    scaled = (w * np.exp2(127.0 - byte)[:, None, :]).reshape(k, n).astype(np.float32)
    words = np.ascontiguousarray(scaled.reshape(k // 512, 128, 4, n).transpose(0, 1, 3, 2)).astype(ml_dtypes.float8_e4m3fn).view(np.uint8)
    return words, np.ascontiguousarray(byte.astype(np.uint8).reshape(k // 512, 16, n))


def unpack_weight(words, scales):
    g, p, n, _ = words.shape
    vals = np.ascontiguousarray(words).view(ml_dtypes.float8_e4m3fn).astype(np.float64) * np.repeat(np.exp2(scales.astype(np.float64) - 127.0), 8, axis=1)[..., None]
    return vals.transpose(0, 1, 3, 2).reshape(g * 512, n)

def planes(y):
    n, m = y.shape
    v = y.astype(np.float32).astype(ml_dtypes.bfloat16).astype(np.float64).reshape(n // 32, 32, m)
    top = np.abs(v).max(1)
    byte = np.clip(np.where(top > 0, np.frexp(top)[1] - 1 + 127 - 7, 1), 1, 254)
    codes = (v * np.exp2(127.0 - byte)[:, None, :]).reshape(n, m).astype(np.float32).astype(ml_dtypes.float8_e4m3fn).view(np.uint8)
    words = codes.reshape(n // 512, 128, 4, m).transpose(0, 1, 3, 2)
    return np.ascontiguousarray(words), np.ascontiguousarray(byte.astype(np.uint8).reshape(n // 512, 16, m))


K, T, N, U = 512, 512, 512, 1024


def setup_inputs():
    n = np.random.standard_normal
    s = mx_kscale(K)[:, None]
    packed_xT = pack_weight(n((K, T)) * s)
    return {
        "x_words": packed_xT[0],
        "x_scales": packed_xT[1],
        "mem": n((N, U)).astype(np.float32),
        "w1": (n((K, N)) / np.sqrt(K) / s).astype(np.float32),
        "slot": striped(np.random.permutation(U)[:T]),
    }


def reference(x_words, x_scales, mem, w1, slot):
    xq = unpack_weight(x_words, x_scales)
    y = mxq(f64(w1), 0, "e4m3").T @ xq
    out = f64(mem).copy()
    out[:, unstriped(slot)] = np.maximum(f64(mem)[:, unstriped(slot)], y)
    return (out,) + planes(out)

@@ -1,0 +1,125 @@
+from contextlib import ExitStack
+
+import concourse.mybir as mybir
+
+K, T, N, U = 512, 512, 512, 1024
+FLOPS = 2 * K * N * T
+
+F32 = mybir.dt.float32
+BF16 = mybir.dt.bfloat16
+I32 = mybir.dt.int32
+U32 = mybir.dt.uint32
+U16 = mybir.dt.uint16
+U8 = mybir.dt.uint8
+FP8X4 = mybir.dt.float8_e4m3fn_x4
+
+P = 128
+PACK = 4
+QUADS = 4
+W_SPLIT = 88
+HALF = U // 2
+
+
+def tile_picked_widxput_max_lo_kernel(tc, x_words, x_scales, mem, w1, slot, out_0, out_1, out_2):
+    nc = tc.nc
+    with ExitStack() as ctx:
+        keep = ctx.enter_context(tc.tile_pool(name="keep", bufs=1))
+        psum = ctx.enter_context(tc.psum_pool(name="psum", bufs=1))
+
+        offsets = keep.tile([P, T // 16], U16, name="offsets")
+        x_codes = keep.tile([P, T], U32, name="x_codes", align_bytes=64)
+        x_plane = keep.tile([P, T], U8, name="x_plane", align_bytes=64)
+        w_raw = [keep.tile([P, 2, N], F32, name="w_raw%d" % h) for h in range(2)]
+        w_bf = keep.tile([P, PACK, P, PACK], BF16, name="w_bf", align_bytes=64)
+        w_codes = [keep.tile([P, P], U32, name="w_codes%d" % t, align_bytes=64) for t in range(PACK)]
+        w_plane = [keep.tile([P, P], U8, name="w_plane%d" % t, align_bytes=64) for t in range(PACK)]
+        store = [keep.tile([P, U], F32, name="store%d" % t) for t in range(PACK)]
+        old = [keep.tile([P, T], F32, name="old%d" % t) for t in range(PACK)]
+        new = [keep.tile([P, T], F32, name="new%d" % t) for t in range(PACK)]
+        y = [psum.tile([P, T], F32, name="y%d" % t) for t in range(PACK)]
+        o_bf = [keep.tile([P, HALF, PACK], BF16, name="o_bf%d" % h, align_bytes=64) for h in range(2)]
+        o_codes = [keep.tile([P, HALF], U32, name="o_codes%d" % h, align_bytes=64) for h in range(2)]
+        o_plane = keep.tile([P, U], U8, name="o_plane", align_bytes=64)
+
+        w_rows = w1.rearrange("(p j) c -> p j c", j=PACK)
+        mem_rows = mem.rearrange("(p t) u -> p t u", t=PACK)
+        out_rows = out_0.rearrange("(p t) u -> p t u", t=PACK)
+
+        nc.vector.memset(x_plane[:].bitcast(U32), 0)
+        for h in range(2):
+            nc.sync.dma_start(out=w_raw[h][:], in_=w_rows[:, 2 * h : 2 * h + 2, :])
+        for q in range(QUADS):
+            nc.scalar.dma_start(
+                out=x_plane[32 * q : 32 * q + 4, :].bitcast(I32),
+                in_=x_scales[0, 4 * q : 4 * q + 4, :].bitcast(I32),
+            )
+        nc.sync.dma_start(offsets[:], slot)
+        nc.sync.dma_start(out=store[0][:], in_=mem_rows[:, 0, :])
+        nc.sync.dma_start(out=x_codes[:].bitcast(I32), in_=x_words[0].rearrange("p c r -> p (c r)").bitcast(I32))
+        for t in range(1, PACK):
+            nc.sync.dma_start(out=store[t][:], in_=mem_rows[:, t, :])
+
+        w_dst = w_bf[:].rearrange("p t m j -> p m j t")
+        w_src = [w_raw[h][:].rearrange("p j (m t) -> p m j t", t=PACK) for h in range(2)]
+        nc.vector.tensor_copy(out=w_dst[:, :, 0:2, :], in_=w_src[0])
+        nc.vector.tensor_copy(out=w_dst[:, :W_SPLIT, 2:4, :], in_=w_src[1][:, :W_SPLIT])
+        nc.scalar.copy(out=w_dst[:, W_SPLIT:, 2:4, :], in_=w_src[1][:, W_SPLIT:])
+
+        def product(t):
+            nc.vector.quantize_mx(
+                out=w_codes[t][:].bitcast(FP8X4),
+                scales=w_plane[t][:],
+                in_=w_bf[:, t].rearrange("p m j -> p (m j)"),
+            )
+            nc.tensor.matmul_mx(
+                out=y[t][:],
+                lhsT=w_codes[t][:].bitcast(FP8X4),
+                lhsT_scale=w_plane[t][:],
+                rhs=x_codes[:].bitcast(FP8X4),
+                rhs_scale=x_plane[:],
+                start=True,
+                stop=True,
+            )
+
+        def look_up(t):
+            nc.vector.tensor_copy(old[t][:], store[t][:].indirect(offsets[:]))
+
+        def larger(t):
+            nc.vector.tensor_tensor(new[t][:], y[t][:], old[t][:], mybir.AluOpType.max)
+
+        def put(t):
+            nc.vector.tensor_copy(store[t][:].indirect(offsets[:]), new[t][:])
+            nc.sync.dma_start(out=out_rows[:, t, :], in_=store[t][:])
+            for h in range(2):
+                src = store[t][:, h * HALF : (h + 1) * HALF]
+                if t == PACK - 1 and h == 0:
+                    nc.vector.tensor_copy(out=o_bf[h][:, :, t], in_=src)
+                elif t == PACK - 2 and h == 0:
+                    nc.scalar.copy(out=o_bf[h][:, :, t:], in_=src.unsqueeze(2).to_broadcast([P, HALF, 2]))
+                else:
+                    nc.scalar.copy(out=o_bf[h][:, :, t], in_=src)
+
+        for t in range(PACK):
+            product(t)
+        look_up(0)
+        for t in range(PACK):
+            larger(t)
+            if t + 1 < PACK:
+                look_up(t + 1)
+            put(t)
+
+        out_words = out_1[0].rearrange("p c r -> p (c r)").bitcast(I32)
+        for h in range(2):
+            cols = slice(h * HALF, (h + 1) * HALF)
+            nc.vector.quantize_mx(
+                out=o_codes[h][:].bitcast(FP8X4),
+                scales=o_plane[:, cols],
+                in_=o_bf[h][:].rearrange("p c t -> p (c t)"),
+            )
+            nc.sync.dma_start(out=out_words[:, cols], in_=o_codes[h][:].bitcast(I32))
+        for q in range(QUADS):
+            queue = nc.scalar if q % 2 == 0 else nc.sync
+            queue.dma_start(
+                out=out_2[0, 4 * q : 4 * q + 4, :].bitcast(I32),
+                in_=o_plane[32 * q : 32 * q + 4, :].bitcast(I32),
+            )

@@ -17,7 +17,9 @@ P = 128
 PACK = 4
 QUADS = 4
 W_SPLIT = 88
-HALF = U // 2
+PARTS = 4
+PART = U // PARTS
+ON_VECTOR = 2
 
 
 def tile_picked_widxput_max_lo_kernel(tc, x_words, x_scales, mem, w1, slot, out_0, out_1, out_2):
@@ -31,14 +33,14 @@ def tile_picked_widxput_max_lo_kernel(tc, x_words, x_scales, mem, w1, slot, out_
         x_plane = keep.tile([P, T], U8, name="x_plane", align_bytes=64)
         w_raw = [keep.tile([P, 2, N], F32, name="w_raw%d" % h) for h in range(2)]
         w_bf = keep.tile([P, PACK, P, PACK], BF16, name="w_bf", align_bytes=64)
-        w_codes = [keep.tile([P, P], U32, name="w_codes%d" % t, align_bytes=64) for t in range(PACK)]
-        w_plane = [keep.tile([P, P], U8, name="w_plane%d" % t, align_bytes=64) for t in range(PACK)]
+        w_codes = keep.tile([P, N], U32, name="w_codes", align_bytes=64)
+        w_plane = keep.tile([P, N], U8, name="w_plane", align_bytes=64)
         store = [keep.tile([P, U], F32, name="store%d" % t) for t in range(PACK)]
         old = [keep.tile([P, T], F32, name="old%d" % t) for t in range(PACK)]
         new = [keep.tile([P, T], F32, name="new%d" % t) for t in range(PACK)]
         y = [psum.tile([P, T], F32, name="y%d" % t) for t in range(PACK)]
-        o_bf = [keep.tile([P, HALF, PACK], BF16, name="o_bf%d" % h, align_bytes=64) for h in range(2)]
-        o_codes = [keep.tile([P, HALF], U32, name="o_codes%d" % h, align_bytes=64) for h in range(2)]
+        o_bf = keep.tile([P, U, PACK], BF16, name="o_bf", align_bytes=64)
+        o_codes = keep.tile([P, U], U32, name="o_codes", align_bytes=64)
         o_plane = keep.tile([P, U], U8, name="o_plane", align_bytes=64)
 
         w_rows = w1.rearrange("(p j) c -> p j c", j=PACK)
@@ -46,18 +48,17 @@ def tile_picked_widxput_max_lo_kernel(tc, x_words, x_scales, mem, w1, slot, out_
         out_rows = out_0.rearrange("(p t) u -> p t u", t=PACK)
 
         nc.vector.memset(x_plane[:].bitcast(U32), 0)
-        for h in range(2):
-            nc.sync.dma_start(out=w_raw[h][:], in_=w_rows[:, 2 * h : 2 * h + 2, :])
+        nc.sync.dma_start(out=w_raw[0][:], in_=w_rows[:, 0:2, :])
         for q in range(QUADS):
-            nc.scalar.dma_start(
+            nc.sync.dma_start(
                 out=x_plane[32 * q : 32 * q + 4, :].bitcast(I32),
                 in_=x_scales[0, 4 * q : 4 * q + 4, :].bitcast(I32),
             )
+        nc.sync.dma_start(out=w_raw[1][:], in_=w_rows[:, 2:4, :])
         nc.sync.dma_start(offsets[:], slot)
-        nc.sync.dma_start(out=store[0][:], in_=mem_rows[:, 0, :])
-        nc.sync.dma_start(out=x_codes[:].bitcast(I32), in_=x_words[0].rearrange("p c r -> p (c r)").bitcast(I32))
-        for t in range(1, PACK):
+        for t in range(PACK):
             nc.sync.dma_start(out=store[t][:], in_=mem_rows[:, t, :])
+        nc.sync.dma_start(out=x_codes[:].bitcast(I32), in_=x_words[0].rearrange("p c r -> p (c r)").bitcast(I32))
 
         w_dst = w_bf[:].rearrange("p t m j -> p m j t")
         w_src = [w_raw[h][:].rearrange("p j (m t) -> p m j t", t=PACK) for h in range(2)]
@@ -65,16 +66,17 @@ def tile_picked_widxput_max_lo_kernel(tc, x_words, x_scales, mem, w1, slot, out_
         nc.vector.tensor_copy(out=w_dst[:, :W_SPLIT, 2:4, :], in_=w_src[1][:, :W_SPLIT])
         nc.scalar.copy(out=w_dst[:, W_SPLIT:, 2:4, :], in_=w_src[1][:, W_SPLIT:])
 
+        nc.vector.quantize_mx(
+            out=w_codes[:].bitcast(FP8X4),
+            scales=w_plane[:],
+            in_=w_bf[:].rearrange("p t m j -> p (t m j)"),
+        )
+
         def product(t):
-            nc.vector.quantize_mx(
-                out=w_codes[t][:].bitcast(FP8X4),
-                scales=w_plane[t][:],
-                in_=w_bf[:, t].rearrange("p m j -> p (m j)"),
-            )
             nc.tensor.matmul_mx(
                 out=y[t][:],
-                lhsT=w_codes[t][:].bitcast(FP8X4),
-                lhsT_scale=w_plane[t][:],
+                lhsT=w_codes[:, t * P : (t + 1) * P].bitcast(FP8X4),
+                lhsT_scale=w_plane[:, t * P : (t + 1) * P],
                 rhs=x_codes[:].bitcast(FP8X4),
                 rhs_scale=x_plane[:],
                 start=True,
@@ -90,33 +92,41 @@ def tile_picked_widxput_max_lo_kernel(tc, x_words, x_scales, mem, w1, slot, out_
         def put(t):
             nc.vector.tensor_copy(store[t][:].indirect(offsets[:]), new[t][:])
             nc.sync.dma_start(out=out_rows[:, t, :], in_=store[t][:])
-            for h in range(2):
-                src = store[t][:, h * HALF : (h + 1) * HALF]
-                if t == PACK - 1 and h == 0:
-                    nc.vector.tensor_copy(out=o_bf[h][:, :, t], in_=src)
-                elif t == PACK - 2 and h == 0:
-                    nc.scalar.copy(out=o_bf[h][:, :, t:], in_=src.unsqueeze(2).to_broadcast([P, HALF, 2]))
-                else:
-                    nc.scalar.copy(out=o_bf[h][:, :, t], in_=src)
+            half = ON_VECTOR * PART
+            if t < PACK - 2:
+                nc.scalar.copy(out=o_bf[:, :, t], in_=store[t][:])
+            elif t == PACK - 2:
+                nc.scalar.copy(out=o_bf[:, :half, t:], in_=store[t][:, :half].unsqueeze(2).to_broadcast([P, half, 2]))
+                nc.scalar.copy(out=o_bf[:, half:, t], in_=store[t][:, half:])
+            else:
+                for h in range(PARTS):
+                    cols = slice(h * PART, (h + 1) * PART)
+                    if h < ON_VECTOR:
+                        nc.vector.tensor_copy(out=o_bf[:, cols, t], in_=store[t][:, cols])
+                    else:
+                        nc.scalar.copy(out=o_bf[:, cols, t], in_=store[t][:, cols])
 
         for t in range(PACK):
-            product(t)
-        look_up(0)
+            look_up(t)
         for t in range(PACK):
-            larger(t)
+            product(t)
+        larger(0)
+        for t in range(PACK):
             if t + 1 < PACK:
-                look_up(t + 1)
+                larger(t + 1)
             put(t)
 
         out_words = out_1[0].rearrange("p c r -> p (c r)").bitcast(I32)
-        for h in range(2):
-            cols = slice(h * HALF, (h + 1) * HALF)
+        for h in range(PARTS):
+            cols = slice(h * PART, (h + 1) * PART)
             nc.vector.quantize_mx(
-                out=o_codes[h][:].bitcast(FP8X4),
+                out=o_codes[:, cols].bitcast(FP8X4),
                 scales=o_plane[:, cols],
-                in_=o_bf[h][:].rearrange("p c t -> p (c t)"),
+                in_=o_bf[:, cols, :].rearrange("p c t -> p (c t)"),
             )
-            nc.sync.dma_start(out=out_words[:, cols], in_=o_codes[h][:].bitcast(I32))
+            if h > 0:
+                cols = slice(0 if h == 1 else h * PART, (h + 1) * PART)
+                nc.sync.dma_start(out=out_words[:, cols], in_=o_codes[:, cols].bitcast(I32))
         for q in range(QUADS):
             queue = nc.scalar if q % 2 == 0 else nc.sync
             queue.dma_start(

@@ -32,13 +32,14 @@ def tile_picked_widxput_max_lo_kernel(tc, x_words, x_scales, mem, w1, slot, out_
         x_codes = keep.tile([P, T], U32, name="x_codes", align_bytes=64)
         x_plane = keep.tile([P, T], U8, name="x_plane", align_bytes=64)
         w_raw = [keep.tile([P, 2, N], F32, name="w_raw%d" % h) for h in range(2)]
-        w_bf = keep.tile([P, PACK, P, PACK], BF16, name="w_bf", align_bytes=64)
+        w_bf = [keep.tile([P, 2, P, PACK], BF16, name="w_bf%d" % u, align_bytes=64) for u in range(2)]
         w_codes = keep.tile([P, N], U32, name="w_codes", align_bytes=64)
         w_plane = keep.tile([P, N], U8, name="w_plane", align_bytes=64)
         store = [keep.tile([P, U], F32, name="store%d" % t) for t in range(PACK)]
-        old = [keep.tile([P, T], F32, name="old%d" % t) for t in range(PACK)]
         new = [keep.tile([P, T], F32, name="new%d" % t) for t in range(PACK)]
-        y = [psum.tile([P, T], F32, name="y%d" % t) for t in range(PACK)]
+        halves = [slice(0, T // 2), slice(T // 2, T)]
+        pieces = [(t, cols) for t in range(2) for cols in halves] + [(t, slice(0, T)) for t in range(2, PACK)]
+        y = [psum.tile([P, cols.stop - cols.start], F32, name="y%d" % i) for i, (t, cols) in enumerate(pieces)]
         o_bf = keep.tile([P, U, PACK], BF16, name="o_bf", align_bytes=64)
         o_codes = keep.tile([P, U], U32, name="o_codes", align_bytes=64)
         o_plane = keep.tile([P, U], U8, name="o_plane", align_bytes=64)
@@ -48,46 +49,60 @@ def tile_picked_widxput_max_lo_kernel(tc, x_words, x_scales, mem, w1, slot, out_
         out_rows = out_0.rearrange("(p t) u -> p t u", t=PACK)
 
         nc.vector.memset(x_plane[:].bitcast(U32), 0)
-        nc.sync.dma_start(out=w_raw[0][:], in_=w_rows[:, 0:2, :])
+        nc.sync.dma_start(out=store[0][:], in_=mem_rows[:, 0, :])
+        nc.sync.dma_start(offsets[:], slot)
+        for h in range(2):
+            nc.sync.dma_start(out=w_raw[h][:], in_=w_rows[:, 2 * h : 2 * h + 2, :])
+        nc.sync.dma_start(out=store[1][:], in_=mem_rows[:, 1, :])
         for q in range(QUADS):
             nc.sync.dma_start(
                 out=x_plane[32 * q : 32 * q + 4, :].bitcast(I32),
                 in_=x_scales[0, 4 * q : 4 * q + 4, :].bitcast(I32),
             )
-        nc.sync.dma_start(out=w_raw[1][:], in_=w_rows[:, 2:4, :])
-        nc.sync.dma_start(offsets[:], slot)
-        for t in range(PACK):
-            nc.sync.dma_start(out=store[t][:], in_=mem_rows[:, t, :])
         nc.sync.dma_start(out=x_codes[:].bitcast(I32), in_=x_words[0].rearrange("p c r -> p (c r)").bitcast(I32))
+        for t in range(2, PACK):
+            nc.sync.dma_start(out=store[t][:], in_=mem_rows[:, t, :])
 
-        w_dst = w_bf[:].rearrange("p t m j -> p m j t")
+        old = {}
+
+        def look_up(t):
+            tag = "w_bf0" if t == 1 else "old%d" % t
+            old[t] = keep.tile([P, T], F32, name="old%d" % t, tag=tag, align_bytes=64)
+            nc.vector.tensor_copy(old[t][:], store[t][:].indirect(offsets[:]))
+
+        look_up(0)
+        w_dst = [w_bf[u][:].rearrange("p t m j -> p m j t") for u in range(2)]
         w_src = [w_raw[h][:].rearrange("p j (m t) -> p m j t", t=PACK) for h in range(2)]
-        nc.vector.tensor_copy(out=w_dst[:, :, 0:2, :], in_=w_src[0])
-        nc.vector.tensor_copy(out=w_dst[:, :W_SPLIT, 2:4, :], in_=w_src[1][:, :W_SPLIT])
-        nc.scalar.copy(out=w_dst[:, W_SPLIT:, 2:4, :], in_=w_src[1][:, W_SPLIT:])
+        for h in range(2):
+            rows = slice(2 * h, 2 * h + 2)
+            for u in range(2):
+                pair = slice(2 * u, 2 * u + 2)
+                nc.vector.tensor_copy(out=w_dst[u][:, :W_SPLIT, rows, :], in_=w_src[h][:, :W_SPLIT, :, pair])
+                nc.scalar.copy(out=w_dst[u][:, W_SPLIT:, rows, :], in_=w_src[h][:, W_SPLIT:, :, pair])
+        for u in range(2):
+            cols = slice(2 * u * P, (2 * u + 2) * P)
+            nc.vector.quantize_mx(
+                out=w_codes[:, cols].bitcast(FP8X4),
+                scales=w_plane[:, cols],
+                in_=w_bf[u][:].rearrange("p t m j -> p (t m j)"),
+            )
 
-        nc.vector.quantize_mx(
-            out=w_codes[:].bitcast(FP8X4),
-            scales=w_plane[:],
-            in_=w_bf[:].rearrange("p t m j -> p (t m j)"),
-        )
-
-        def product(t):
+        def product(i):
+            t, cols = pieces[i]
             nc.tensor.matmul_mx(
-                out=y[t][:],
+                out=y[i][:],
                 lhsT=w_codes[:, t * P : (t + 1) * P].bitcast(FP8X4),
                 lhsT_scale=w_plane[:, t * P : (t + 1) * P],
-                rhs=x_codes[:].bitcast(FP8X4),
-                rhs_scale=x_plane[:],
+                rhs=x_codes[:, cols].bitcast(FP8X4),
+                rhs_scale=x_plane[:, cols],
                 start=True,
                 stop=True,
             )
 
-        def look_up(t):
-            nc.vector.tensor_copy(old[t][:], store[t][:].indirect(offsets[:]))
-
         def larger(t):
-            nc.vector.tensor_tensor(new[t][:], y[t][:], old[t][:], mybir.AluOpType.max)
+            for i, (owner, cols) in enumerate(pieces):
+                if owner == t:
+                    nc.vector.tensor_tensor(new[t][:, cols], y[i][:], old[t][:, cols], mybir.AluOpType.max)
 
         def put(t):
             nc.vector.tensor_copy(store[t][:].indirect(offsets[:]), new[t][:])
@@ -106,15 +121,19 @@ def tile_picked_widxput_max_lo_kernel(tc, x_words, x_scales, mem, w1, slot, out_
                     else:
                         nc.scalar.copy(out=o_bf[:, cols, t], in_=store[t][:, cols])
 
-        for t in range(PACK):
-            look_up(t)
-        for t in range(PACK):
-            product(t)
+        look_up(1)
+        for i in range(len(pieces)):
+            product(i)
         larger(0)
-        for t in range(PACK):
-            if t + 1 < PACK:
-                larger(t + 1)
-            put(t)
+        larger(1)
+        put(0)
+        look_up(2)
+        put(1)
+        look_up(3)
+        larger(2)
+        larger(3)
+        put(2)
+        put(3)
 
         out_words = out_1[0].rearrange("p c r -> p (c r)").bitcast(I32)
         for h in range(PARTS):

@@ -15,11 +15,15 @@ FP8X4 = mybir.dt.float8_e4m3fn_x4
 
 P = 128
 PACK = 4
-QUADS = 4
-W_SPLIT = 88
-PARTS = 4
-PART = U // PARTS
-ON_VECTOR = 2
+QUADRANTS = 4
+
+ORDER = (0, 2, 1, 3)
+
+W_ON_VECTOR = (88, 48)
+
+PART = 256
+LAST_ON_VECTOR = 2 * PART
+THIRD_ON_VECTOR = 128
 
 
 def tile_picked_widxput_max_lo_kernel(tc, x_words, x_scales, mem, w1, slot, out_0, out_1, out_2):
@@ -30,74 +34,34 @@ def tile_picked_widxput_max_lo_kernel(tc, x_words, x_scales, mem, w1, slot, out_
 
         offsets = keep.tile([P, T // 16], U16, name="offsets")
         x_codes = keep.tile([P, T], U32, name="x_codes", align_bytes=64)
-        x_plane = keep.tile([P, T], U8, name="x_plane", align_bytes=64)
+        x_scale = keep.tile([P, T], U8, name="x_scale", align_bytes=64)
         w_raw = [keep.tile([P, 2, N], F32, name="w_raw%d" % h) for h in range(2)]
         w_bf = [keep.tile([P, 2, P, PACK], BF16, name="w_bf%d" % u, align_bytes=64) for u in range(2)]
         w_codes = keep.tile([P, N], U32, name="w_codes", align_bytes=64)
-        w_plane = keep.tile([P, N], U8, name="w_plane", align_bytes=64)
+        w_scale = keep.tile([P, N], U8, name="w_scale", align_bytes=64)
         store = [keep.tile([P, U], F32, name="store%d" % t) for t in range(PACK)]
         new = [keep.tile([P, T], F32, name="new%d" % t) for t in range(PACK)]
-        halves = [slice(0, T // 2), slice(T // 2, T)]
-        pieces = [(t, cols) for t in range(2) for cols in halves] + [(t, slice(0, T)) for t in range(2, PACK)]
-        y = [psum.tile([P, cols.stop - cols.start], F32, name="y%d" % i) for i, (t, cols) in enumerate(pieces)]
         o_bf = keep.tile([P, U, PACK], BF16, name="o_bf", align_bytes=64)
         o_codes = keep.tile([P, U], U32, name="o_codes", align_bytes=64)
-        o_plane = keep.tile([P, U], U8, name="o_plane", align_bytes=64)
+        o_scale = keep.tile([P, U], U8, name="o_scale", align_bytes=64)
+        old = {}
+
+        halves = [slice(0, T // 2), slice(T // 2, T)]
+        pieces = [(t, cols) for t in ORDER[:2] for cols in halves] + [(t, slice(0, T)) for t in ORDER[2:]]
+        y = [psum.tile([P, cols.stop - cols.start], F32, name="y%d" % i) for i, (t, cols) in enumerate(pieces)]
 
         w_rows = w1.rearrange("(p j) c -> p j c", j=PACK)
         mem_rows = mem.rearrange("(p t) u -> p t u", t=PACK)
         out_rows = out_0.rearrange("(p t) u -> p t u", t=PACK)
+        out_words = out_1[0].rearrange("p c r -> p (c r)").bitcast(I32)
 
-        nc.vector.memset(x_plane[:].bitcast(U32), 0)
-        nc.sync.dma_start(out=store[0][:], in_=mem_rows[:, 0, :])
-        nc.sync.dma_start(offsets[:], slot)
-        for h in range(2):
-            nc.sync.dma_start(out=w_raw[h][:], in_=w_rows[:, 2 * h : 2 * h + 2, :])
-        nc.sync.dma_start(out=store[1][:], in_=mem_rows[:, 1, :])
-        for q in range(QUADS):
-            nc.sync.dma_start(
-                out=x_plane[32 * q : 32 * q + 4, :].bitcast(I32),
-                in_=x_scales[0, 4 * q : 4 * q + 4, :].bitcast(I32),
-            )
-        nc.sync.dma_start(out=x_codes[:].bitcast(I32), in_=x_words[0].rearrange("p c r -> p (c r)").bitcast(I32))
-        for t in range(2, PACK):
+        def load_set(t):
             nc.sync.dma_start(out=store[t][:], in_=mem_rows[:, t, :])
 
-        old = {}
-
         def look_up(t):
-            tag = "w_bf0" if t == 1 else "old%d" % t
+            tag = "w_bf0" if t == ORDER[1] else "old%d" % t
             old[t] = keep.tile([P, T], F32, name="old%d" % t, tag=tag, align_bytes=64)
             nc.vector.tensor_copy(old[t][:], store[t][:].indirect(offsets[:]))
-
-        look_up(0)
-        w_dst = [w_bf[u][:].rearrange("p t m j -> p m j t") for u in range(2)]
-        w_src = [w_raw[h][:].rearrange("p j (m t) -> p m j t", t=PACK) for h in range(2)]
-        for h in range(2):
-            rows = slice(2 * h, 2 * h + 2)
-            for u in range(2):
-                pair = slice(2 * u, 2 * u + 2)
-                nc.vector.tensor_copy(out=w_dst[u][:, :W_SPLIT, rows, :], in_=w_src[h][:, :W_SPLIT, :, pair])
-                nc.scalar.copy(out=w_dst[u][:, W_SPLIT:, rows, :], in_=w_src[h][:, W_SPLIT:, :, pair])
-        for u in range(2):
-            cols = slice(2 * u * P, (2 * u + 2) * P)
-            nc.vector.quantize_mx(
-                out=w_codes[:, cols].bitcast(FP8X4),
-                scales=w_plane[:, cols],
-                in_=w_bf[u][:].rearrange("p t m j -> p (t m j)"),
-            )
-
-        def product(i):
-            t, cols = pieces[i]
-            nc.tensor.matmul_mx(
-                out=y[i][:],
-                lhsT=w_codes[:, t * P : (t + 1) * P].bitcast(FP8X4),
-                lhsT_scale=w_plane[:, t * P : (t + 1) * P],
-                rhs=x_codes[:, cols].bitcast(FP8X4),
-                rhs_scale=x_plane[:, cols],
-                start=True,
-                stop=True,
-            )
 
         def larger(t):
             for i, (owner, cols) in enumerate(pieces):
@@ -107,48 +71,92 @@ def tile_picked_widxput_max_lo_kernel(tc, x_words, x_scales, mem, w1, slot, out_
         def put(t):
             nc.vector.tensor_copy(store[t][:].indirect(offsets[:]), new[t][:])
             nc.sync.dma_start(out=out_rows[:, t, :], in_=store[t][:])
-            half = ON_VECTOR * PART
-            if t < PACK - 2:
-                nc.scalar.copy(out=o_bf[:, :, t], in_=store[t][:])
-            elif t == PACK - 2:
-                nc.scalar.copy(out=o_bf[:, :half, t:], in_=store[t][:, :half].unsqueeze(2).to_broadcast([P, half, 2]))
-                nc.scalar.copy(out=o_bf[:, half:, t], in_=store[t][:, half:])
+
+        def round_even(t, shared):
+            both = store[t][:, :shared].unsqueeze(2).to_broadcast([P, shared, 2])
+            nc.scalar.copy(out=o_bf[:, :shared, t : t + 2], in_=both)
+            nc.scalar.copy(out=o_bf[:, shared:, t], in_=store[t][:, shared:])
+
+        nc.vector.memset(x_scale[:].bitcast(U32), 0)
+        load_set(ORDER[0])
+        nc.sync.dma_start(offsets[:], slot)
+        for h in range(2):
+            nc.sync.dma_start(out=w_raw[h][:], in_=w_rows[:, 2 * h : 2 * h + 2, :])
+        load_set(ORDER[1])
+        for q in range(QUADRANTS):
+            nc.sync.dma_start(
+                out=x_scale[32 * q : 32 * q + 4, :].bitcast(I32),
+                in_=x_scales[0, 4 * q : 4 * q + 4, :].bitcast(I32),
+            )
+        nc.sync.dma_start(out=x_codes[:].bitcast(I32), in_=x_words[0].rearrange("p c r -> p (c r)").bitcast(I32))
+        for t in ORDER[2:]:
+            load_set(t)
+
+        look_up(ORDER[0])
+
+        for h in range(2):
+            for u in range(2):
+                dst = w_bf[u][:].rearrange("p i m j -> p m j i")[:, :, 2 * h : 2 * h + 2, :]
+                src = w_raw[h][:].rearrange("p j (m i u) -> p m j i u", i=2, u=2)[:, :, :, :, u]
+                split = W_ON_VECTOR[u]
+                nc.vector.tensor_copy(out=dst[:, :split], in_=src[:, :split])
+                nc.scalar.copy(out=dst[:, split:], in_=src[:, split:])
+        for u in range(2):
+            cols = slice(2 * u * P, (2 * u + 2) * P)
+            nc.vector.quantize_mx(
+                out=w_codes[:, cols].bitcast(FP8X4),
+                scales=w_scale[:, cols],
+                in_=w_bf[u][:].rearrange("p i m j -> p (i m j)"),
+            )
+
+        look_up(ORDER[1])
+        for i, (t, cols) in enumerate(pieces):
+            w_cols = slice(ORDER.index(t) * P, (ORDER.index(t) + 1) * P)
+            nc.tensor.matmul_mx(
+                out=y[i][:],
+                lhsT=w_codes[:, w_cols].bitcast(FP8X4),
+                lhsT_scale=w_scale[:, w_cols],
+                rhs=x_codes[:, cols].bitcast(FP8X4),
+                rhs_scale=x_scale[:, cols],
+                start=True,
+                stop=True,
+            )
+
+        first, second, third, last = ORDER
+        larger(first)
+        larger(second)
+        put(first)
+        round_even(first, THIRD_ON_VECTOR)
+        look_up(third)
+        put(second)
+        round_even(second, LAST_ON_VECTOR)
+        look_up(last)
+        larger(third)
+        larger(last)
+        put(third)
+        nc.scalar.copy(out=o_bf[:, THIRD_ON_VECTOR:, third], in_=store[third][:, THIRD_ON_VECTOR:])
+        put(last)
+        nc.vector.tensor_copy(out=o_bf[:, :THIRD_ON_VECTOR, third], in_=store[third][:, :THIRD_ON_VECTOR])
+
+        parts = [slice(c, c + PART) for c in range(0, U, PART)]
+        for cols in parts:
+            if cols.stop <= LAST_ON_VECTOR:
+                nc.vector.tensor_copy(out=o_bf[:, cols, last], in_=store[last][:, cols])
             else:
-                for h in range(PARTS):
-                    cols = slice(h * PART, (h + 1) * PART)
-                    if h < ON_VECTOR:
-                        nc.vector.tensor_copy(out=o_bf[:, cols, t], in_=store[t][:, cols])
-                    else:
-                        nc.scalar.copy(out=o_bf[:, cols, t], in_=store[t][:, cols])
+                nc.scalar.copy(out=o_bf[:, cols, last], in_=store[last][:, cols])
 
-        look_up(1)
-        for i in range(len(pieces)):
-            product(i)
-        larger(0)
-        larger(1)
-        put(0)
-        look_up(2)
-        put(1)
-        look_up(3)
-        larger(2)
-        larger(3)
-        put(2)
-        put(3)
-
-        out_words = out_1[0].rearrange("p c r -> p (c r)").bitcast(I32)
-        for h in range(PARTS):
-            cols = slice(h * PART, (h + 1) * PART)
+        for cols in parts:
             nc.vector.quantize_mx(
                 out=o_codes[:, cols].bitcast(FP8X4),
-                scales=o_plane[:, cols],
+                scales=o_scale[:, cols],
                 in_=o_bf[:, cols, :].rearrange("p c t -> p (c t)"),
             )
-            if h > 0:
-                cols = slice(0 if h == 1 else h * PART, (h + 1) * PART)
-                nc.sync.dma_start(out=out_words[:, cols], in_=o_codes[:, cols].bitcast(I32))
-        for q in range(QUADS):
+            if cols.stop >= LAST_ON_VECTOR:
+                done = slice(0 if cols.stop == LAST_ON_VECTOR else cols.start, cols.stop)
+                nc.sync.dma_start(out=out_words[:, done], in_=o_codes[:, done].bitcast(I32))
+        for q in range(QUADRANTS):
             queue = nc.scalar if q % 2 == 0 else nc.sync
             queue.dma_start(
                 out=out_2[0, 4 * q : 4 * q + 4, :].bitcast(I32),
-                in_=o_plane[32 * q : 32 * q + 4, :].bitcast(I32),
+                in_=o_scale[32 * q : 32 * q + 4, :].bitcast(I32),
             )

@@ -84,7 +84,7 @@ def tile_picked_widxput_max_lo_kernel(tc, x_words, x_scales, mem, w1, slot, out_
             nc.sync.dma_start(out=w_raw[h][:], in_=w_rows[:, 2 * h : 2 * h + 2, :])
         load_set(ORDER[1])
         for q in range(QUADRANTS):
-            nc.sync.dma_start(
+            nc.scalar.dma_start(
                 out=x_scale[32 * q : 32 * q + 4, :].bitcast(I32),
                 in_=x_scales[0, 4 * q : 4 * q + 4, :].bitcast(I32),
             )

@@ -41,7 +41,6 @@ def tile_picked_widxput_max_lo_kernel(tc, x_words, x_scales, mem, w1, slot, out_
         w_scale = keep.tile([P, N], U8, name="w_scale", align_bytes=64)
         store = [keep.tile([P, U], F32, name="store%d" % t) for t in range(PACK)]
         new = [keep.tile([P, T], F32, name="new%d" % t) for t in range(PACK)]
-        o_bf = keep.tile([P, U, PACK], BF16, name="o_bf", align_bytes=64)
         o_codes = keep.tile([P, U], U32, name="o_codes", align_bytes=64)
         o_scale = keep.tile([P, U], U8, name="o_scale", align_bytes=64)
         old = {}
@@ -68,8 +67,34 @@ def tile_picked_widxput_max_lo_kernel(tc, x_words, x_scales, mem, w1, slot, out_
                 if owner == t:
                     nc.vector.tensor_tensor(new[t][:, cols], y[i][:], old[t][:, cols], mybir.AluOpType.max)
 
+        work = {}
+
+        def difference(t):
+            work[t] = [keep.tile([P, T], F32, name="work%d_%d" % (t, i), align_bytes=64) for i in range(6)]
+            y_sb, diff = work[t][0], work[t][1]
+            nc.scalar.copy(out=y_sb[:], in_=y[[owner for owner, cols in pieces].index(t)][:])
+            nc.gpsimd.tensor_tensor(diff[:], y_sb[:], old[t][:], mybir.AluOpType.subtract)
+
+        def masks(t):
+            y_sb, diff, sign, take_y, take_old, part = work[t]
+            nc.scalar.activation(sign[:], diff[:], mybir.ActivationFunctionType.Sign)
+            nc.scalar.activation(take_y[:], sign[:], mybir.ActivationFunctionType.Relu)
+            nc.scalar.activation(take_old[:], take_y[:], mybir.ActivationFunctionType.Copy, bias=1.0, scale=-1.0)
+
+        def select(t):
+            y_sb, diff, sign, take_y, take_old, part = work[t]
+            nc.gpsimd.tensor_tensor(part[:], y_sb[:], take_y[:], mybir.AluOpType.mult)
+            if t == ORDER[3]:
+                nc.gpsimd.tensor_tensor(new[t][:], old[t][:], take_old[:], mybir.AluOpType.mult)
+            else:
+                nc.gpsimd.tensor_tensor(diff[:], old[t][:], take_old[:], mybir.AluOpType.mult)
+                nc.gpsimd.tensor_tensor(new[t][:], part[:], diff[:], mybir.AluOpType.add)
+
         def put(t):
-            nc.vector.tensor_copy(store[t][:].indirect(offsets[:]), new[t][:])
+            if t == ORDER[3]:
+                nc.vector.tensor_tensor(store[t][:].indirect(offsets[:]), new[t][:], work[t][5][:], mybir.AluOpType.add)
+            else:
+                nc.vector.tensor_copy(store[t][:].indirect(offsets[:]), new[t][:])
             nc.sync.dma_start(out=out_rows[:, t, :], in_=store[t][:])
 
         def round_even(t, shared):
@@ -83,14 +108,14 @@ def tile_picked_widxput_max_lo_kernel(tc, x_words, x_scales, mem, w1, slot, out_
         for h in range(2):
             nc.sync.dma_start(out=w_raw[h][:], in_=w_rows[:, 2 * h : 2 * h + 2, :])
         load_set(ORDER[1])
+        load_set(ORDER[2])
         for q in range(QUADRANTS):
             nc.scalar.dma_start(
                 out=x_scale[32 * q : 32 * q + 4, :].bitcast(I32),
                 in_=x_scales[0, 4 * q : 4 * q + 4, :].bitcast(I32),
             )
         nc.sync.dma_start(out=x_codes[:].bitcast(I32), in_=x_words[0].rearrange("p c r -> p (c r)").bitcast(I32))
-        for t in ORDER[2:]:
-            load_set(t)
+        load_set(ORDER[3])
 
         look_up(ORDER[0])
 
@@ -110,6 +135,7 @@ def tile_picked_widxput_max_lo_kernel(tc, x_words, x_scales, mem, w1, slot, out_
             )
 
         look_up(ORDER[1])
+        look_up(ORDER[2])
         for i, (t, cols) in enumerate(pieces):
             w_cols = slice(ORDER.index(t) * P, (ORDER.index(t) + 1) * P)
             nc.tensor.matmul_mx(
@@ -125,14 +151,19 @@ def tile_picked_widxput_max_lo_kernel(tc, x_words, x_scales, mem, w1, slot, out_
         first, second, third, last = ORDER
         larger(first)
         larger(second)
-        put(first)
-        round_even(first, THIRD_ON_VECTOR)
-        look_up(third)
-        put(second)
-        round_even(second, LAST_ON_VECTOR)
         look_up(last)
         larger(third)
-        larger(last)
+        for t in (last,):
+            difference(t)
+        for t in (last,):
+            masks(t)
+        for t in (last,):
+            select(t)
+        o_bf = keep.tile([P, U, PACK], BF16, name="o_bf", tag="work%d_2" % last, align_bytes=64)
+        put(first)
+        round_even(first, THIRD_ON_VECTOR)
+        put(second)
+        round_even(second, LAST_ON_VECTOR)
         put(third)
         nc.scalar.copy(out=o_bf[:, THIRD_ON_VECTOR:, third], in_=store[third][:, THIRD_ON_VECTOR:])
         put(last)

@@ -18,9 +18,7 @@ PACK = 4
 QUADRANTS = 4
 
 ORDER = (0, 2, 1, 3)
-
 W_ON_VECTOR = (88, 48)
-
 PART = 256
 LAST_ON_VECTOR = 2 * PART
 THIRD_ON_VECTOR = 128
@@ -28,9 +26,13 @@ THIRD_ON_VECTOR = 128
 
 def tile_picked_widxput_max_lo_kernel(tc, x_words, x_scales, mem, w1, slot, out_0, out_1, out_2):
     nc = tc.nc
+    first, second, third, last = ORDER
     with ExitStack() as ctx:
         keep = ctx.enter_context(tc.tile_pool(name="keep", bufs=1))
         psum = ctx.enter_context(tc.psum_pool(name="psum", bufs=1))
+
+        def values(name, tag=None):
+            return keep.tile([P, T], F32, name=name, tag=tag or name, align_bytes=64)
 
         offsets = keep.tile([P, T // 16], U16, name="offsets")
         x_codes = keep.tile([P, T], U32, name="x_codes", align_bytes=64)
@@ -40,14 +42,13 @@ def tile_picked_widxput_max_lo_kernel(tc, x_words, x_scales, mem, w1, slot, out_
         w_codes = keep.tile([P, N], U32, name="w_codes", align_bytes=64)
         w_scale = keep.tile([P, N], U8, name="w_scale", align_bytes=64)
         store = [keep.tile([P, U], F32, name="store%d" % t) for t in range(PACK)]
-        new = [keep.tile([P, T], F32, name="new%d" % t) for t in range(PACK)]
         o_codes = keep.tile([P, U], U32, name="o_codes", align_bytes=64)
         o_scale = keep.tile([P, U], U8, name="o_scale", align_bytes=64)
-        old = {}
+        old, new, y_sb, diff, sign, take_y, take_old, from_y, from_old = ({} for i in range(9))
 
+        whole = slice(0, T)
         halves = [slice(0, T // 2), slice(T // 2, T)]
-        pieces = [(t, cols) for t in ORDER[:2] for cols in halves] + [(t, slice(0, T)) for t in ORDER[2:]]
-        y = [psum.tile([P, cols.stop - cols.start], F32, name="y%d" % i) for i, (t, cols) in enumerate(pieces)]
+        y = [psum.tile([P, T], F32, name="y%d" % t) for t in range(PACK)]
 
         w_rows = w1.rearrange("(p j) c -> p j c", j=PACK)
         mem_rows = mem.rearrange("(p t) u -> p t u", t=PACK)
@@ -57,44 +58,42 @@ def tile_picked_widxput_max_lo_kernel(tc, x_words, x_scales, mem, w1, slot, out_
         def load_set(t):
             nc.sync.dma_start(out=store[t][:], in_=mem_rows[:, t, :])
 
-        def look_up(t):
-            tag = "w_bf0" if t == ORDER[1] else "old%d" % t
-            old[t] = keep.tile([P, T], F32, name="old%d" % t, tag=tag, align_bytes=64)
-            nc.vector.tensor_copy(old[t][:], store[t][:].indirect(offsets[:]))
+        def look_up(t, pieces):
+            old[t] = values("old%d" % t, "w_bf0" if t == first else None)
+            for cols in pieces:
+                entries = offsets[:, cols.start // 16 : cols.stop // 16]
+                nc.vector.tensor_copy(old[t][:, cols], store[t][:].indirect(entries))
 
-        def larger(t):
-            for i, (owner, cols) in enumerate(pieces):
-                if owner == t:
-                    nc.vector.tensor_tensor(new[t][:, cols], y[i][:], old[t][:, cols], mybir.AluOpType.max)
+        def larger(t, pieces):
+            new[t] = values("new%d" % t)
+            for cols in pieces:
+                nc.vector.tensor_tensor(new[t][:, cols], y[t][:, cols], old[t][:, cols], mybir.AluOpType.max)
 
-        work = {}
+        def compare(t):
+            y_sb[t], diff[t] = values("y_sb%d" % t), values("diff%d" % t)
+            nc.scalar.copy(out=y_sb[t][:], in_=y[t][:])
+            nc.gpsimd.tensor_tensor(diff[t][:], y_sb[t][:], old[t][:], mybir.AluOpType.subtract)
 
-        def difference(t):
-            work[t] = [keep.tile([P, T], F32, name="work%d_%d" % (t, i), align_bytes=64) for i in range(6)]
-            y_sb, diff = work[t][0], work[t][1]
-            nc.scalar.copy(out=y_sb[:], in_=y[[owner for owner, cols in pieces].index(t)][:])
-            nc.gpsimd.tensor_tensor(diff[:], y_sb[:], old[t][:], mybir.AluOpType.subtract)
-
-        def masks(t):
-            y_sb, diff, sign, take_y, take_old, part = work[t]
-            nc.scalar.activation(sign[:], diff[:], mybir.ActivationFunctionType.Sign)
-            nc.scalar.activation(take_y[:], sign[:], mybir.ActivationFunctionType.Relu)
-            nc.scalar.activation(take_old[:], take_y[:], mybir.ActivationFunctionType.Copy, bias=1.0, scale=-1.0)
+        def decide(t):
+            sign[t], take_y[t], take_old[t] = values("sign%d" % t), values("take_y%d" % t), values("take_old%d" % t)
+            nc.scalar.activation(sign[t][:], diff[t][:], mybir.ActivationFunctionType.Sign)
+            nc.scalar.activation(take_y[t][:], sign[t][:], mybir.ActivationFunctionType.Relu)
+            nc.scalar.activation(take_old[t][:], take_y[t][:], mybir.ActivationFunctionType.Copy, bias=1.0, scale=-1.0)
 
         def select(t):
-            y_sb, diff, sign, take_y, take_old, part = work[t]
-            nc.gpsimd.tensor_tensor(part[:], y_sb[:], take_y[:], mybir.AluOpType.mult)
-            if t == ORDER[3]:
-                nc.gpsimd.tensor_tensor(new[t][:], old[t][:], take_old[:], mybir.AluOpType.mult)
-            else:
-                nc.gpsimd.tensor_tensor(diff[:], old[t][:], take_old[:], mybir.AluOpType.mult)
-                nc.gpsimd.tensor_tensor(new[t][:], part[:], diff[:], mybir.AluOpType.add)
+            from_y[t], from_old[t] = values("from_y%d" % t, "from_y"), values("from_old%d" % t)
+            nc.gpsimd.tensor_tensor(from_y[t][:], y_sb[t][:], take_y[t][:], mybir.AluOpType.mult)
+            nc.gpsimd.tensor_tensor(from_old[t][:], old[t][:], take_old[t][:], mybir.AluOpType.mult)
+            if t == third:
+                new[t] = values("new%d" % t)
+                nc.gpsimd.tensor_tensor(new[t][:], from_y[t][:], from_old[t][:], mybir.AluOpType.add)
 
         def put(t):
-            if t == ORDER[3]:
-                nc.vector.tensor_tensor(store[t][:].indirect(offsets[:]), new[t][:], work[t][5][:], mybir.AluOpType.add)
+            window = store[t][:].indirect(offsets[:])
+            if t == last:
+                nc.vector.tensor_tensor(window, from_y[t][:], from_old[t][:], mybir.AluOpType.add)
             else:
-                nc.vector.tensor_copy(store[t][:].indirect(offsets[:]), new[t][:])
+                nc.vector.tensor_copy(window, new[t][:])
             nc.sync.dma_start(out=out_rows[:, t, :], in_=store[t][:])
 
         def round_even(t, shared):
@@ -103,22 +102,21 @@ def tile_picked_widxput_max_lo_kernel(tc, x_words, x_scales, mem, w1, slot, out_
             nc.scalar.copy(out=o_bf[:, shared:, t], in_=store[t][:, shared:])
 
         nc.vector.memset(x_scale[:].bitcast(U32), 0)
-        load_set(ORDER[0])
+        load_set(third)
         nc.sync.dma_start(offsets[:], slot)
         for h in range(2):
             nc.sync.dma_start(out=w_raw[h][:], in_=w_rows[:, 2 * h : 2 * h + 2, :])
-        load_set(ORDER[1])
-        load_set(ORDER[2])
+        load_set(first)
         for q in range(QUADRANTS):
             nc.scalar.dma_start(
                 out=x_scale[32 * q : 32 * q + 4, :].bitcast(I32),
                 in_=x_scales[0, 4 * q : 4 * q + 4, :].bitcast(I32),
             )
         nc.sync.dma_start(out=x_codes[:].bitcast(I32), in_=x_words[0].rearrange("p c r -> p (c r)").bitcast(I32))
-        load_set(ORDER[3])
+        load_set(last)
+        load_set(second)
 
-        look_up(ORDER[0])
-
+        look_up(third, [whole])
         for h in range(2):
             for u in range(2):
                 dst = w_bf[u][:].rearrange("p i m j -> p m j i")[:, :, 2 * h : 2 * h + 2, :]
@@ -134,34 +132,30 @@ def tile_picked_widxput_max_lo_kernel(tc, x_words, x_scales, mem, w1, slot, out_
                 in_=w_bf[u][:].rearrange("p i m j -> p (i m j)"),
             )
 
-        look_up(ORDER[1])
-        look_up(ORDER[2])
-        for i, (t, cols) in enumerate(pieces):
+        look_up(first, [whole])
+        for t in (first, third, last, second):
             w_cols = slice(ORDER.index(t) * P, (ORDER.index(t) + 1) * P)
             nc.tensor.matmul_mx(
-                out=y[i][:],
+                out=y[t][:],
                 lhsT=w_codes[:, w_cols].bitcast(FP8X4),
                 lhsT_scale=w_scale[:, w_cols],
-                rhs=x_codes[:, cols].bitcast(FP8X4),
-                rhs_scale=x_scale[:, cols],
+                rhs=x_codes[:].bitcast(FP8X4),
+                rhs_scale=x_scale[:],
                 start=True,
                 stop=True,
             )
 
-        first, second, third, last = ORDER
-        larger(first)
-        larger(second)
-        look_up(last)
-        larger(third)
-        for t in (last,):
-            difference(t)
-        for t in (last,):
-            masks(t)
-        for t in (last,):
-            select(t)
-        o_bf = keep.tile([P, U, PACK], BF16, name="o_bf", tag="work%d_2" % last, align_bytes=64)
+        larger(first, [whole])
+        look_up(last, [whole])
+        for step in (compare, decide, select):
+            for t in (third, last):
+                step(t)
+
+        o_bf = keep.tile([P, U, PACK], BF16, name="o_bf", tag="sign%d" % last, align_bytes=64)
         put(first)
         round_even(first, THIRD_ON_VECTOR)
+        look_up(second, halves)
+        larger(second, halves)
         put(second)
         round_even(second, LAST_ON_VECTOR)
         put(third)

@@ -21,7 +21,6 @@ ORDER = (0, 2, 1, 3)
 W_ON_VECTOR = (88, 48)
 PART = 256
 LAST_ON_VECTOR = 2 * PART
-THIRD_ON_VECTOR = 128
 
 
 def tile_picked_widxput_max_lo_kernel(tc, x_words, x_scales, mem, w1, slot, out_0, out_1, out_2):
@@ -75,14 +74,17 @@ def tile_picked_widxput_max_lo_kernel(tc, x_words, x_scales, mem, w1, slot, out_
             nc.gpsimd.tensor_tensor(diff[t][:], y_sb[t][:], old[t][:], mybir.AluOpType.subtract)
 
         def decide(t):
-            sign[t], take_y[t], take_old[t] = values("sign%d" % t), values("take_y%d" % t), values("take_old%d" % t)
+            sign[t], take_y[t], take_old[t] = values("sign%d" % t, "sign"), values("take_y%d" % t), values("take_old%d" % t, "take_old")
             nc.scalar.activation(sign[t][:], diff[t][:], mybir.ActivationFunctionType.Sign)
             nc.scalar.activation(take_y[t][:], sign[t][:], mybir.ActivationFunctionType.Relu)
-            nc.scalar.activation(take_old[t][:], take_y[t][:], mybir.ActivationFunctionType.Copy, bias=1.0, scale=-1.0)
+            if t == third:
+                nc.scalar.activation(take_old[t][:], take_y[t][:], mybir.ActivationFunctionType.Copy, bias=1.0, scale=-1.0)
 
         def select(t):
-            from_y[t], from_old[t] = values("from_y%d" % t, "from_y"), values("from_old%d" % t)
+            from_y[t], from_old[t] = values("from_y%d" % t, "from_y"), values("from_old%d" % t, "from_old")
             nc.gpsimd.tensor_tensor(from_y[t][:], y_sb[t][:], take_y[t][:], mybir.AluOpType.mult)
+            if t == last:
+                nc.gpsimd.tensor_scalar(take_old[t][:], take_y[t][:], -1.0, 1.0, mybir.AluOpType.mult, mybir.AluOpType.add)
             nc.gpsimd.tensor_tensor(from_old[t][:], old[t][:], take_old[t][:], mybir.AluOpType.mult)
             if t == third:
                 new[t] = values("new%d" % t)
@@ -151,17 +153,16 @@ def tile_picked_widxput_max_lo_kernel(tc, x_words, x_scales, mem, w1, slot, out_
             for t in (third, last):
                 step(t)
 
-        o_bf = keep.tile([P, U, PACK], BF16, name="o_bf", tag="sign%d" % last, align_bytes=64)
+        o_bf = keep.tile([P, U, PACK], BF16, name="o_bf", tag="sign", align_bytes=64)
         put(first)
-        round_even(first, THIRD_ON_VECTOR)
+        nc.scalar.copy(out=o_bf[:, :, first], in_=store[first][:])
         look_up(second, halves)
         larger(second, halves)
         put(second)
         round_even(second, LAST_ON_VECTOR)
         put(third)
-        nc.scalar.copy(out=o_bf[:, THIRD_ON_VECTOR:, third], in_=store[third][:, THIRD_ON_VECTOR:])
+        nc.scalar.copy(out=o_bf[:, :, third], in_=store[third][:])
         put(last)
-        nc.vector.tensor_copy(out=o_bf[:, :THIRD_ON_VECTOR, third], in_=store[third][:, :THIRD_ON_VECTOR])
 
         parts = [slice(c, c + PART) for c in range(0, U, PART)]
         for cols in parts:

@@ -19,8 +19,10 @@ QUADRANTS = 4
 
 ORDER = (0, 2, 1, 3)
 W_ON_VECTOR = (88, 48)
-PART = 256
-LAST_ON_VECTOR = 2 * PART
+PARTS = (0, 256, 512, 768, 896, 1024)
+STORES = (512, 896, 1024,)
+VECTOR_CUTS = (0, 256, 480)
+LAST_ON_VECTOR = 480
 
 
 def tile_picked_widxput_max_lo_kernel(tc, x_words, x_scales, mem, w1, slot, out_0, out_1, out_2):
@@ -103,7 +105,6 @@ def tile_picked_widxput_max_lo_kernel(tc, x_words, x_scales, mem, w1, slot, out_
             nc.scalar.copy(out=o_bf[:, :shared, t : t + 2], in_=both)
             nc.scalar.copy(out=o_bf[:, shared:, t], in_=store[t][:, shared:])
 
-        nc.vector.memset(x_scale[:].bitcast(U32), 0)
         load_set(third)
         nc.sync.dma_start(offsets[:], slot)
         for h in range(2):
@@ -122,7 +123,7 @@ def tile_picked_widxput_max_lo_kernel(tc, x_words, x_scales, mem, w1, slot, out_
         for h in range(2):
             for u in range(2):
                 dst = w_bf[u][:].rearrange("p i m j -> p m j i")[:, :, 2 * h : 2 * h + 2, :]
-                src = w_raw[h][:].rearrange("p j (m i u) -> p m j i u", i=2, u=2)[:, :, :, :, u]
+                src = w_raw[h][:].rearrange("p j (m t) -> p m j t", t=PACK)[:, :, :, 2 * u : 2 * u + 2]
                 split = W_ON_VECTOR[u]
                 nc.vector.tensor_copy(out=dst[:, :split], in_=src[:, :split])
                 nc.scalar.copy(out=dst[:, split:], in_=src[:, split:])
@@ -136,7 +137,7 @@ def tile_picked_widxput_max_lo_kernel(tc, x_words, x_scales, mem, w1, slot, out_
 
         look_up(first, [whole])
         for t in (first, third, last, second):
-            w_cols = slice(ORDER.index(t) * P, (ORDER.index(t) + 1) * P)
+            w_cols = slice(t * P, (t + 1) * P)
             nc.tensor.matmul_mx(
                 out=y[t][:],
                 lhsT=w_codes[:, w_cols].bitcast(FP8X4),
@@ -164,22 +165,22 @@ def tile_picked_widxput_max_lo_kernel(tc, x_words, x_scales, mem, w1, slot, out_
         nc.scalar.copy(out=o_bf[:, :, third], in_=store[third][:])
         put(last)
 
-        parts = [slice(c, c + PART) for c in range(0, U, PART)]
-        for cols in parts:
-            if cols.stop <= LAST_ON_VECTOR:
-                nc.vector.tensor_copy(out=o_bf[:, cols, last], in_=store[last][:, cols])
-            else:
-                nc.scalar.copy(out=o_bf[:, cols, last], in_=store[last][:, cols])
+        for a, b in zip(VECTOR_CUTS, VECTOR_CUTS[1:]):
+            nc.vector.tensor_copy(out=o_bf[:, a:b, last], in_=store[last][:, a:b])
+        scalar_cuts = [LAST_ON_VECTOR] + [c for c in PARTS if c > LAST_ON_VECTOR]
+        for a, b in zip(scalar_cuts, scalar_cuts[1:]):
+            nc.scalar.copy(out=o_bf[:, a:b, last], in_=store[last][:, a:b])
 
-        for cols in parts:
+        stored = 0
+        for a, b in zip(PARTS, PARTS[1:]):
             nc.vector.quantize_mx(
-                out=o_codes[:, cols].bitcast(FP8X4),
-                scales=o_scale[:, cols],
-                in_=o_bf[:, cols, :].rearrange("p c t -> p (c t)"),
+                out=o_codes[:, a:b].bitcast(FP8X4),
+                scales=o_scale[:, a:b],
+                in_=o_bf[:, a:b, :].rearrange("p c t -> p (c t)"),
             )
-            if cols.stop >= LAST_ON_VECTOR:
-                done = slice(0 if cols.stop == LAST_ON_VECTOR else cols.start, cols.stop)
-                nc.sync.dma_start(out=out_words[:, done], in_=o_codes[:, done].bitcast(I32))
+            if b in STORES:
+                nc.sync.dma_start(out=out_words[:, stored:b], in_=o_codes[:, stored:b].bitcast(I32))
+                stored = b
         for q in range(QUADRANTS):
             queue = nc.scalar if q % 2 == 0 else nc.sync
             queue.dma_start(

@@ -12,17 +12,23 @@ U32 = mybir.dt.uint32
 U16 = mybir.dt.uint16
 U8 = mybir.dt.uint8
 FP8X4 = mybir.dt.float8_e4m3fn_x4
+ALU = mybir.AluOpType
+ACT = mybir.ActivationFunctionType
 
 P = 128
 PACK = 4
 QUADRANTS = 4
+STRIPE = 16
 
 ORDER = (0, 2, 1, 3)
-W_ON_VECTOR = (88, 48)
-PARTS = (0, 256, 512, 768, 896, 1024)
-STORES = (512, 896, 1024,)
-VECTOR_CUTS = (0, 256, 480)
-LAST_ON_VECTOR = 480
+
+W_ON_VECTOR = 88
+
+LAST_ON_VECTOR = U // 2
+
+PARTS = (0, U // 4, U // 2, 3 * U // 4, 7 * U // 8, U)
+
+STORE_AT = (U // 2, 7 * U // 8, U)
 
 
 def tile_picked_widxput_max_lo_kernel(tc, x_words, x_scales, mem, w1, slot, out_0, out_1, out_2):
@@ -32,10 +38,10 @@ def tile_picked_widxput_max_lo_kernel(tc, x_words, x_scales, mem, w1, slot, out_
         keep = ctx.enter_context(tc.tile_pool(name="keep", bufs=1))
         psum = ctx.enter_context(tc.psum_pool(name="psum", bufs=1))
 
-        def values(name, tag=None):
+        def per_entry(name, tag=None):
             return keep.tile([P, T], F32, name=name, tag=tag or name, align_bytes=64)
 
-        offsets = keep.tile([P, T // 16], U16, name="offsets")
+        offsets = keep.tile([P, T // STRIPE], U16, name="offsets")
         x_codes = keep.tile([P, T], U32, name="x_codes", align_bytes=64)
         x_scale = keep.tile([P, T], U8, name="x_scale", align_bytes=64)
         w_raw = [keep.tile([P, 2, N], F32, name="w_raw%d" % h) for h in range(2)]
@@ -47,7 +53,7 @@ def tile_picked_widxput_max_lo_kernel(tc, x_words, x_scales, mem, w1, slot, out_
         o_scale = keep.tile([P, U], U8, name="o_scale", align_bytes=64)
         old, new, y_sb, diff, sign, take_y, take_old, from_y, from_old = ({} for i in range(9))
 
-        whole = slice(0, T)
+        whole = [slice(0, T)]
         halves = [slice(0, T // 2), slice(T // 2, T)]
         y = [psum.tile([P, T], F32, name="y%d" % t) for t in range(PACK)]
 
@@ -60,50 +66,46 @@ def tile_picked_widxput_max_lo_kernel(tc, x_words, x_scales, mem, w1, slot, out_
             nc.sync.dma_start(out=store[t][:], in_=mem_rows[:, t, :])
 
         def look_up(t, pieces):
-            old[t] = values("old%d" % t, "w_bf0" if t == first else None)
+            old[t] = per_entry("old%d" % t, "w_bf0" if t == first else None)
             for cols in pieces:
-                entries = offsets[:, cols.start // 16 : cols.stop // 16]
+                entries = offsets[:, cols.start // STRIPE : cols.stop // STRIPE]
                 nc.vector.tensor_copy(old[t][:, cols], store[t][:].indirect(entries))
 
         def larger(t, pieces):
-            new[t] = values("new%d" % t)
+            new[t] = per_entry("new%d" % t)
             for cols in pieces:
-                nc.vector.tensor_tensor(new[t][:, cols], y[t][:, cols], old[t][:, cols], mybir.AluOpType.max)
+                nc.vector.tensor_tensor(new[t][:, cols], y[t][:, cols], old[t][:, cols], ALU.max)
 
         def compare(t):
-            y_sb[t], diff[t] = values("y_sb%d" % t), values("diff%d" % t)
+            y_sb[t], diff[t] = per_entry("y_sb%d" % t), per_entry("diff%d" % t)
             nc.scalar.copy(out=y_sb[t][:], in_=y[t][:])
-            nc.gpsimd.tensor_tensor(diff[t][:], y_sb[t][:], old[t][:], mybir.AluOpType.subtract)
+            nc.gpsimd.tensor_tensor(diff[t][:], y_sb[t][:], old[t][:], ALU.subtract)
 
         def decide(t):
-            sign[t], take_y[t], take_old[t] = values("sign%d" % t, "sign"), values("take_y%d" % t), values("take_old%d" % t, "take_old")
-            nc.scalar.activation(sign[t][:], diff[t][:], mybir.ActivationFunctionType.Sign)
-            nc.scalar.activation(take_y[t][:], sign[t][:], mybir.ActivationFunctionType.Relu)
+            sign[t], take_y[t] = per_entry("sign%d" % t, "sign"), per_entry("take_y%d" % t)
+            take_old[t] = per_entry("take_old%d" % t, "take_old")
+            nc.scalar.activation(sign[t][:], diff[t][:], ACT.Sign)
+            nc.scalar.activation(take_y[t][:], sign[t][:], ACT.Relu)
             if t == third:
-                nc.scalar.activation(take_old[t][:], take_y[t][:], mybir.ActivationFunctionType.Copy, bias=1.0, scale=-1.0)
+                nc.scalar.activation(take_old[t][:], take_y[t][:], ACT.Copy, bias=1.0, scale=-1.0)
 
         def select(t):
-            from_y[t], from_old[t] = values("from_y%d" % t, "from_y"), values("from_old%d" % t, "from_old")
-            nc.gpsimd.tensor_tensor(from_y[t][:], y_sb[t][:], take_y[t][:], mybir.AluOpType.mult)
+            from_y[t], from_old[t] = per_entry("from_y%d" % t, "from_y"), per_entry("from_old%d" % t, "from_old")
+            nc.gpsimd.tensor_tensor(from_y[t][:], y_sb[t][:], take_y[t][:], ALU.mult)
             if t == last:
-                nc.gpsimd.tensor_scalar(take_old[t][:], take_y[t][:], -1.0, 1.0, mybir.AluOpType.mult, mybir.AluOpType.add)
-            nc.gpsimd.tensor_tensor(from_old[t][:], old[t][:], take_old[t][:], mybir.AluOpType.mult)
+                nc.gpsimd.tensor_scalar(take_old[t][:], take_y[t][:], -1.0, 1.0, ALU.mult, ALU.add)
+            nc.gpsimd.tensor_tensor(from_old[t][:], old[t][:], take_old[t][:], ALU.mult)
             if t == third:
-                new[t] = values("new%d" % t)
-                nc.gpsimd.tensor_tensor(new[t][:], from_y[t][:], from_old[t][:], mybir.AluOpType.add)
+                new[t] = per_entry("new%d" % t)
+                nc.gpsimd.tensor_tensor(new[t][:], from_y[t][:], from_old[t][:], ALU.add)
 
         def put(t):
             window = store[t][:].indirect(offsets[:])
             if t == last:
-                nc.vector.tensor_tensor(window, from_y[t][:], from_old[t][:], mybir.AluOpType.add)
+                nc.vector.tensor_tensor(window, from_y[t][:], from_old[t][:], ALU.add)
             else:
                 nc.vector.tensor_copy(window, new[t][:])
             nc.sync.dma_start(out=out_rows[:, t, :], in_=store[t][:])
-
-        def round_even(t, shared):
-            both = store[t][:, :shared].unsqueeze(2).to_broadcast([P, shared, 2])
-            nc.scalar.copy(out=o_bf[:, :shared, t : t + 2], in_=both)
-            nc.scalar.copy(out=o_bf[:, shared:, t], in_=store[t][:, shared:])
 
         load_set(third)
         nc.sync.dma_start(offsets[:], slot)
@@ -119,13 +121,15 @@ def tile_picked_widxput_max_lo_kernel(tc, x_words, x_scales, mem, w1, slot, out_
         load_set(last)
         load_set(second)
 
-        look_up(third, [whole])
+        look_up(third, whole)
+
         for h in range(2):
             for u in range(2):
                 dst = w_bf[u][:].rearrange("p i m j -> p m j i")[:, :, 2 * h : 2 * h + 2, :]
                 src = w_raw[h][:].rearrange("p j (m t) -> p m j t", t=PACK)[:, :, :, 2 * u : 2 * u + 2]
-                split = W_ON_VECTOR[u]
-                nc.vector.tensor_copy(out=dst[:, :split], in_=src[:, :split])
+                split = W_ON_VECTOR if u == 0 else 0
+                if split:
+                    nc.vector.tensor_copy(out=dst[:, :split], in_=src[:, :split])
                 nc.scalar.copy(out=dst[:, split:], in_=src[:, split:])
         for u in range(2):
             cols = slice(2 * u * P, (2 * u + 2) * P)
@@ -135,7 +139,7 @@ def tile_picked_widxput_max_lo_kernel(tc, x_words, x_scales, mem, w1, slot, out_
                 in_=w_bf[u][:].rearrange("p i m j -> p (i m j)"),
             )
 
-        look_up(first, [whole])
+        look_up(first, whole)
         for t in (first, third, last, second):
             w_cols = slice(t * P, (t + 1) * P)
             nc.tensor.matmul_mx(
@@ -148,8 +152,8 @@ def tile_picked_widxput_max_lo_kernel(tc, x_words, x_scales, mem, w1, slot, out_
                 stop=True,
             )
 
-        larger(first, [whole])
-        look_up(last, [whole])
+        larger(first, whole)
+        look_up(last, whole)
         for step in (compare, decide, select):
             for t in (third, last):
                 step(t)
@@ -157,30 +161,36 @@ def tile_picked_widxput_max_lo_kernel(tc, x_words, x_scales, mem, w1, slot, out_
         o_bf = keep.tile([P, U, PACK], BF16, name="o_bf", tag="sign", align_bytes=64)
         put(first)
         nc.scalar.copy(out=o_bf[:, :, first], in_=store[first][:])
+
         look_up(second, halves)
         larger(second, halves)
         put(second)
-        round_even(second, LAST_ON_VECTOR)
+
+        both = store[second][:, :LAST_ON_VECTOR].unsqueeze(2).to_broadcast([P, LAST_ON_VECTOR, 2])
+        nc.scalar.copy(out=o_bf[:, :LAST_ON_VECTOR, second : second + 2], in_=both)
+        nc.scalar.copy(out=o_bf[:, LAST_ON_VECTOR:, second], in_=store[second][:, LAST_ON_VECTOR:])
         put(third)
         nc.scalar.copy(out=o_bf[:, :, third], in_=store[third][:])
         put(last)
 
-        for a, b in zip(VECTOR_CUTS, VECTOR_CUTS[1:]):
-            nc.vector.tensor_copy(out=o_bf[:, a:b, last], in_=store[last][:, a:b])
-        scalar_cuts = [LAST_ON_VECTOR] + [c for c in PARTS if c > LAST_ON_VECTOR]
-        for a, b in zip(scalar_cuts, scalar_cuts[1:]):
-            nc.scalar.copy(out=o_bf[:, a:b, last], in_=store[last][:, a:b])
+        parts = [slice(a, b) for a, b in zip(PARTS, PARTS[1:])]
+        for cols in parts:
+            if cols.stop <= LAST_ON_VECTOR:
+                nc.vector.tensor_copy(out=o_bf[:, cols, last], in_=store[last][:, cols])
+            else:
+                nc.scalar.copy(out=o_bf[:, cols, last], in_=store[last][:, cols])
 
         stored = 0
-        for a, b in zip(PARTS, PARTS[1:]):
+        for cols in parts:
             nc.vector.quantize_mx(
-                out=o_codes[:, a:b].bitcast(FP8X4),
-                scales=o_scale[:, a:b],
-                in_=o_bf[:, a:b, :].rearrange("p c t -> p (c t)"),
+                out=o_codes[:, cols].bitcast(FP8X4),
+                scales=o_scale[:, cols],
+                in_=o_bf[:, cols, :].rearrange("p c t -> p (c t)"),
             )
-            if b in STORES:
-                nc.sync.dma_start(out=out_words[:, stored:b], in_=o_codes[:, stored:b].bitcast(I32))
-                stored = b
+            if cols.stop in STORE_AT:
+                nc.sync.dma_start(out=out_words[:, stored : cols.stop], in_=o_codes[:, stored : cols.stop].bitcast(I32))
+                stored = cols.stop
+
         for q in range(QUADRANTS):
             queue = nc.scalar if q % 2 == 0 else nc.sync
             queue.dma_start(

@@ -20,7 +20,7 @@ PACK = 4
 QUADRANTS = 4
 STRIPE = 16
 
-ORDER = (0, 2, 1, 3)
+ORDER = (2, 1, 0, 3)
 
 W_ON_VECTOR = 88
 
@@ -48,10 +48,10 @@ def tile_picked_widxput_max_lo_kernel(tc, x_words, x_scales, mem, w1, slot, out_
         w_bf = [keep.tile([P, 2, P, PACK], BF16, name="w_bf%d" % u, align_bytes=64) for u in range(2)]
         w_codes = keep.tile([P, N], U32, name="w_codes", align_bytes=64)
         w_scale = keep.tile([P, N], U8, name="w_scale", align_bytes=64)
-        store = [keep.tile([P, U], F32, name="store%d" % t) for t in range(PACK)]
+        store = [keep.tile([P, U], F32, name="store%d" % t, align_bytes=64) for t in range(PACK)]
         o_codes = keep.tile([P, U], U32, name="o_codes", align_bytes=64)
         o_scale = keep.tile([P, U], U8, name="o_scale", align_bytes=64)
-        old, new, y_sb, diff, sign, take_y, take_old, from_y, from_old = ({} for i in range(9))
+        old, new, y_sb, diff, sign, take_y, take_old, from_y, from_old = {}, {}, {}, {}, {}, {}, {}, {}, {}
 
         whole = [slice(0, T)]
         halves = [slice(0, T // 2), slice(T // 2, T)]
@@ -90,7 +90,8 @@ def tile_picked_widxput_max_lo_kernel(tc, x_words, x_scales, mem, w1, slot, out_
                 nc.scalar.activation(take_old[t][:], take_y[t][:], ACT.Copy, bias=1.0, scale=-1.0)
 
         def select(t):
-            from_y[t], from_old[t] = per_entry("from_y%d" % t, "from_y"), per_entry("from_old%d" % t, "from_old")
+            from_y[t] = per_entry("from_y%d" % t, "from_y")
+            from_old[t] = per_entry("from_old%d" % t, "store%d" % first if t == last else None)
             nc.gpsimd.tensor_tensor(from_y[t][:], y_sb[t][:], take_y[t][:], ALU.mult)
             if t == last:
                 nc.gpsimd.tensor_scalar(take_old[t][:], take_y[t][:], -1.0, 1.0, ALU.mult, ALU.add)
@@ -126,7 +127,7 @@ def tile_picked_widxput_max_lo_kernel(tc, x_words, x_scales, mem, w1, slot, out_
         for h in range(2):
             for u in range(2):
                 dst = w_bf[u][:].rearrange("p i m j -> p m j i")[:, :, 2 * h : 2 * h + 2, :]
-                src = w_raw[h][:].rearrange("p j (m t) -> p m j t", t=PACK)[:, :, :, 2 * u : 2 * u + 2]
+                src = w_raw[h][:].rearrange("p j (m i u) -> p m j i u", i=2, u=2)[:, :, :, :, u]
                 split = W_ON_VECTOR if u == 0 else 0
                 if split:
                     nc.vector.tensor_copy(out=dst[:, :split], in_=src[:, :split])
@@ -141,7 +142,8 @@ def tile_picked_widxput_max_lo_kernel(tc, x_words, x_scales, mem, w1, slot, out_
 
         look_up(first, whole)
         for t in (first, third, last, second):
-            w_cols = slice(t * P, (t + 1) * P)
+            place = 2 * (t % 2) + t // 2
+            w_cols = slice(place * P, (place + 1) * P)
             nc.tensor.matmul_mx(
                 out=y[t][:],
                 lhsT=w_codes[:, w_cols].bitcast(FP8X4),
@@ -154,21 +156,21 @@ def tile_picked_widxput_max_lo_kernel(tc, x_words, x_scales, mem, w1, slot, out_
 
         larger(first, whole)
         look_up(last, whole)
-        for step in (compare, decide, select):
+        for step in (compare, decide):
             for t in (third, last):
                 step(t)
+        select(third)
 
         o_bf = keep.tile([P, U, PACK], BF16, name="o_bf", tag="sign", align_bytes=64)
         put(first)
         nc.scalar.copy(out=o_bf[:, :, first], in_=store[first][:])
 
+        select(last)
+
         look_up(second, halves)
         larger(second, halves)
         put(second)
-
-        both = store[second][:, :LAST_ON_VECTOR].unsqueeze(2).to_broadcast([P, LAST_ON_VECTOR, 2])
-        nc.scalar.copy(out=o_bf[:, :LAST_ON_VECTOR, second : second + 2], in_=both)
-        nc.scalar.copy(out=o_bf[:, LAST_ON_VECTOR:, second], in_=store[second][:, LAST_ON_VECTOR:])
+        nc.scalar.copy(out=o_bf[:, :, second], in_=store[second][:])
         put(third)
         nc.scalar.copy(out=o_bf[:, :, third], in_=store[third][:])
         put(last)

@@ -19,6 +19,7 @@ P = 128
 PACK = 4
 QUADRANTS = 4
 STRIPE = 16
+F32_MAX = (2.0 - 2.0**-23) * 2.0**127
 
 ORDER = (2, 1, 0, 3)
 
@@ -51,7 +52,7 @@ def tile_picked_widxput_max_lo_kernel(tc, x_words, x_scales, mem, w1, slot, out_
         store = [keep.tile([P, U], F32, name="store%d" % t, align_bytes=64) for t in range(PACK)]
         o_codes = keep.tile([P, U], U32, name="o_codes", align_bytes=64)
         o_scale = keep.tile([P, U], U8, name="o_scale", align_bytes=64)
-        old, new, y_sb, diff, sign, take_y, take_old, from_y, from_old = {}, {}, {}, {}, {}, {}, {}, {}, {}
+        old, new, finite, y_sb, diff, sign, take_y, take_old, from_y, from_old = {}, {}, {}, {}, {}, {}, {}, {}, {}, {}
 
         whole = [slice(0, T)]
         halves = [slice(0, T // 2), slice(T // 2, T)]
@@ -77,9 +78,10 @@ def tile_picked_widxput_max_lo_kernel(tc, x_words, x_scales, mem, w1, slot, out_
                 nc.vector.tensor_tensor(new[t][:, cols], y[t][:, cols], old[t][:, cols], ALU.max)
 
         def compare(t):
-            y_sb[t], diff[t] = per_entry("y_sb%d" % t), per_entry("diff%d" % t)
+            finite[t], y_sb[t], diff[t] = per_entry("finite%d" % t), per_entry("y_sb%d" % t), per_entry("diff%d" % t)
+            nc.gpsimd.tensor_scalar(finite[t][:], old[t][:], F32_MAX, -F32_MAX, ALU.min, ALU.max)
             nc.scalar.copy(out=y_sb[t][:], in_=y[t][:])
-            nc.gpsimd.tensor_tensor(diff[t][:], y_sb[t][:], old[t][:], ALU.subtract)
+            nc.gpsimd.tensor_tensor(diff[t][:], y_sb[t][:], finite[t][:], ALU.subtract)
 
         def decide(t):
             sign[t], take_y[t] = per_entry("sign%d" % t, "sign"), per_entry("take_y%d" % t)
@@ -95,7 +97,7 @@ def tile_picked_widxput_max_lo_kernel(tc, x_words, x_scales, mem, w1, slot, out_
             nc.gpsimd.tensor_tensor(from_y[t][:], y_sb[t][:], take_y[t][:], ALU.mult)
             if t == last:
                 nc.gpsimd.tensor_scalar(take_old[t][:], take_y[t][:], -1.0, 1.0, ALU.mult, ALU.add)
-            nc.gpsimd.tensor_tensor(from_old[t][:], old[t][:], take_old[t][:], ALU.mult)
+            nc.gpsimd.tensor_tensor(from_old[t][:], finite[t][:], take_old[t][:], ALU.mult)
             if t == third:
                 new[t] = per_entry("new%d" % t)
                 nc.gpsimd.tensor_tensor(new[t][:], from_y[t][:], from_old[t][:], ALU.add)

@@ -56,7 +56,8 @@ def tile_picked_widxput_max_lo_kernel(tc, x_words, x_scales, mem, w1, slot, out_
 
         whole = [slice(0, T)]
         halves = [slice(0, T // 2), slice(T // 2, T)]
-        y = [psum.tile([P, T], F32, name="y%d" % t) for t in range(PACK)]
+        y = {t: psum.tile([P, T], F32, name="y%d" % t) for t in (second, third, last)}
+        y_first = [psum.tile([P, T // 2], F32, name="y_first%d" % h) for h in range(2)]
 
         w_rows = w1.rearrange("(p j) c -> p j c", j=PACK)
         mem_rows = mem.rearrange("(p t) u -> p t u", t=PACK)
@@ -71,6 +72,19 @@ def tile_picked_widxput_max_lo_kernel(tc, x_words, x_scales, mem, w1, slot, out_
             for cols in pieces:
                 entries = offsets[:, cols.start // STRIPE : cols.stop // STRIPE]
                 nc.vector.tensor_copy(old[t][:, cols], store[t][:].indirect(entries))
+
+        def product(t, bank, cols):
+            place = 2 * (t % 2) + t // 2
+            w_cols = slice(place * P, (place + 1) * P)
+            nc.tensor.matmul_mx(
+                out=bank,
+                lhsT=w_codes[:, w_cols].bitcast(FP8X4),
+                lhsT_scale=w_scale[:, w_cols],
+                rhs=x_codes[:, cols].bitcast(FP8X4),
+                rhs_scale=x_scale[:, cols],
+                start=True,
+                stop=True,
+            )
 
         def larger(t, pieces):
             new[t] = per_entry("new%d" % t)
@@ -143,20 +157,14 @@ def tile_picked_widxput_max_lo_kernel(tc, x_words, x_scales, mem, w1, slot, out_
             )
 
         look_up(first, whole)
-        for t in (first, third, last, second):
-            place = 2 * (t % 2) + t // 2
-            w_cols = slice(place * P, (place + 1) * P)
-            nc.tensor.matmul_mx(
-                out=y[t][:],
-                lhsT=w_codes[:, w_cols].bitcast(FP8X4),
-                lhsT_scale=w_scale[:, w_cols],
-                rhs=x_codes[:].bitcast(FP8X4),
-                rhs_scale=x_scale[:],
-                start=True,
-                stop=True,
-            )
+        for h, cols in enumerate(halves):
+            product(first, y_first[h][:], cols)
+        for t in (third, last, second):
+            product(t, y[t][:], whole[0])
 
-        larger(first, whole)
+        new[first] = per_entry("new%d" % first)
+        for h, cols in enumerate(halves):
+            nc.vector.tensor_tensor(new[first][:, cols], y_first[h][:], old[first][:, cols], ALU.max)
         look_up(last, whole)
         for step in (compare, decide):
             for t in (third, last):

@@ -199,13 +199,13 @@ def tile_picked_widxput_max_lo_kernel(tc, x_words, x_scales, mem, w1, slot, out_
                 scales=o_scale[:, cols],
                 in_=o_bf[:, cols, :].rearrange("p c t -> p (c t)"),
             )
-            if cols.stop in STORE_AT:
+            if cols.stop in STORE_AT[:-1]:
                 nc.sync.dma_start(out=out_words[:, stored : cols.stop], in_=o_codes[:, stored : cols.stop].bitcast(I32))
                 stored = cols.stop
 
-        for q in range(QUADRANTS):
-            queue = nc.scalar if q % 2 == 0 else nc.sync
+        for q, queue in ((0, nc.scalar), (3, nc.sync), (2, nc.scalar), (1, nc.sync)):
             queue.dma_start(
                 out=out_2[0, 4 * q : 4 * q + 4, :].bitcast(I32),
                 in_=o_scale[32 * q : 32 * q + 4, :].bitcast(I32),
             )
+        nc.sync.dma_start(out=out_words[:, stored:], in_=o_codes[:, stored:].bitcast(I32))

@@ -19,28 +19,17 @@ P = 128
 PACK = 4
 QUADRANTS = 4
 STRIPE = 16
-F32_MAX = (2.0 - 2.0**-23) * 2.0**127
-
-ORDER = (2, 1, 0, 3)
-
+HALF = T // 2
 W_ON_VECTOR = 88
-
-LAST_ON_VECTOR = U // 2
-
-PARTS = (0, U // 4, U // 2, 3 * U // 4, 7 * U // 8, U)
-
-STORE_AT = (U // 2, 7 * U // 8, U)
+PARTS = 4
+PART = U // PARTS
 
 
 def tile_picked_widxput_max_lo_kernel(tc, x_words, x_scales, mem, w1, slot, out_0, out_1, out_2):
     nc = tc.nc
-    first, second, third, last = ORDER
     with ExitStack() as ctx:
         keep = ctx.enter_context(tc.tile_pool(name="keep", bufs=1))
         psum = ctx.enter_context(tc.psum_pool(name="psum", bufs=1))
-
-        def per_entry(name, tag=None):
-            return keep.tile([P, T], F32, name=name, tag=tag or name, align_bytes=64)
 
         offsets = keep.tile([P, T // STRIPE], U16, name="offsets")
         x_codes = keep.tile([P, T], U32, name="x_codes", align_bytes=64)
@@ -50,34 +39,38 @@ def tile_picked_widxput_max_lo_kernel(tc, x_words, x_scales, mem, w1, slot, out_
         w_codes = keep.tile([P, N], U32, name="w_codes", align_bytes=64)
         w_scale = keep.tile([P, N], U8, name="w_scale", align_bytes=64)
         store = [keep.tile([P, U], F32, name="store%d" % t, align_bytes=64) for t in range(PACK)]
+        pairs = [keep.tile([P, 2, PART, 2], BF16, name="pairs%d" % i, align_bytes=64) for i in range(PARTS)]
+        o_bf = [keep.tile([P, PART, PACK], BF16, name="o_bf%d" % i, align_bytes=64) for i in range(PARTS)]
         o_codes = keep.tile([P, U], U32, name="o_codes", align_bytes=64)
         o_scale = keep.tile([P, U], U8, name="o_scale", align_bytes=64)
-        old, new, finite, y_sb, diff, sign, take_y, take_old, from_y, from_old = {}, {}, {}, {}, {}, {}, {}, {}, {}, {}
-
-        whole = [slice(0, T)]
-        halves = [slice(0, T // 2), slice(T // 2, T)]
-        y = {t: psum.tile([P, T], F32, name="y%d" % t) for t in (second, third, last)}
-        y_first = [psum.tile([P, T // 2], F32, name="y_first%d" % h) for h in range(2)]
+        y = {(t, h): psum.tile([P, HALF], F32, name="y%d_%d" % (t, h)) for t in range(PACK) for h in range(2)}
+        old, new = {}, {}
 
         w_rows = w1.rearrange("(p j) c -> p j c", j=PACK)
         mem_rows = mem.rearrange("(p t) u -> p t u", t=PACK)
         out_rows = out_0.rearrange("(p t) u -> p t u", t=PACK)
+        x_rows = x_words[0].rearrange("p c r -> p (c r)").bitcast(I32)
         out_words = out_1[0].rearrange("p c r -> p (c r)").bitcast(I32)
+
+        def entries(h):
+            return offsets[:, h * HALF // STRIPE : (h + 1) * HALF // STRIPE]
 
         def load_set(t):
             nc.sync.dma_start(out=store[t][:], in_=mem_rows[:, t, :])
 
-        def look_up(t, pieces):
-            old[t] = per_entry("old%d" % t, "w_bf0" if t == first else None)
-            for cols in pieces:
-                entries = offsets[:, cols.start // STRIPE : cols.stop // STRIPE]
-                nc.vector.tensor_copy(old[t][:, cols], store[t][:].indirect(entries))
+        def look_up(t, h, on_scalar=False):
+            old[t, h] = keep.tile([P, HALF], F32, name="old%d_%d" % (t, h), align_bytes=64)
+            window = store[t][:].indirect(entries(h))
+            if on_scalar:
+                nc.scalar.activation(old[t, h][:], window, ACT.Copy)
+            else:
+                nc.vector.tensor_copy(old[t, h][:], window)
 
-        def product(t, bank, cols):
-            place = 2 * (t % 2) + t // 2
-            w_cols = slice(place * P, (place + 1) * P)
+        def product(t, h):
+            w_cols = slice(t * P, (t + 1) * P)
+            cols = slice(h * HALF, (h + 1) * HALF)
             nc.tensor.matmul_mx(
-                out=bank,
+                out=y[t, h][:],
                 lhsT=w_codes[:, w_cols].bitcast(FP8X4),
                 lhsT_scale=w_scale[:, w_cols],
                 rhs=x_codes[:, cols].bitcast(FP8X4),
@@ -86,68 +79,61 @@ def tile_picked_widxput_max_lo_kernel(tc, x_words, x_scales, mem, w1, slot, out_
                 stop=True,
             )
 
-        def larger(t, pieces):
-            new[t] = per_entry("new%d" % t)
-            for cols in pieces:
-                nc.vector.tensor_tensor(new[t][:, cols], y[t][:, cols], old[t][:, cols], ALU.max)
+        def larger(t, h, tag=None):
+            name = "new%d_%d" % (t, h)
+            new[t, h] = keep.tile([P, HALF], F32, name=name, tag=tag or name, align_bytes=64)
+            nc.vector.tensor_tensor(new[t, h][:], y[t, h][:], old[t, h][:], ALU.max)
 
-        def compare(t):
-            finite[t], y_sb[t], diff[t] = per_entry("finite%d" % t), per_entry("y_sb%d" % t), per_entry("diff%d" % t)
-            nc.gpsimd.tensor_scalar(finite[t][:], old[t][:], F32_MAX, -F32_MAX, ALU.min, ALU.max)
-            nc.scalar.copy(out=y_sb[t][:], in_=y[t][:])
-            nc.gpsimd.tensor_tensor(diff[t][:], y_sb[t][:], finite[t][:], ALU.subtract)
-
-        def decide(t):
-            sign[t], take_y[t] = per_entry("sign%d" % t, "sign"), per_entry("take_y%d" % t)
-            take_old[t] = per_entry("take_old%d" % t, "take_old")
-            nc.scalar.activation(sign[t][:], diff[t][:], ACT.Sign)
-            nc.scalar.activation(take_y[t][:], sign[t][:], ACT.Relu)
-            if t == third:
-                nc.scalar.activation(take_old[t][:], take_y[t][:], ACT.Copy, bias=1.0, scale=-1.0)
-
-        def select(t):
-            from_y[t] = per_entry("from_y%d" % t, "from_y")
-            from_old[t] = per_entry("from_old%d" % t, "store%d" % first if t == last else None)
-            nc.gpsimd.tensor_tensor(from_y[t][:], y_sb[t][:], take_y[t][:], ALU.mult)
-            if t == last:
-                nc.gpsimd.tensor_scalar(take_old[t][:], take_y[t][:], -1.0, 1.0, ALU.mult, ALU.add)
-            nc.gpsimd.tensor_tensor(from_old[t][:], finite[t][:], take_old[t][:], ALU.mult)
-            if t == third:
-                new[t] = per_entry("new%d" % t)
-                nc.gpsimd.tensor_tensor(new[t][:], from_y[t][:], from_old[t][:], ALU.add)
-
-        def put(t):
-            window = store[t][:].indirect(offsets[:])
-            if t == last:
-                nc.vector.tensor_tensor(window, from_y[t][:], from_old[t][:], ALU.add)
+        def put(t, h, on_scalar):
+            window = store[t][:].indirect(entries(h))
+            if on_scalar:
+                nc.scalar.activation(window, new[t, h][:], ACT.Copy)
             else:
-                nc.vector.tensor_copy(window, new[t][:])
+                nc.vector.tensor_copy(window, new[t, h][:])
+
+        def leave(t):
             nc.sync.dma_start(out=out_rows[:, t, :], in_=store[t][:])
 
-        load_set(third)
-        nc.sync.dma_start(offsets[:], slot)
+        def round_set(t, i):
+            dst = pairs[i][:, t // 2, :, t % 2]
+            src = store[t][:, i * PART : (i + 1) * PART]
+            if t < 2:
+                nc.gpsimd.tensor_scalar(dst, src, 1.0, 1.0, ALU.mult, ALU.mult)
+            else:
+                nc.vector.tensor_copy(out=dst, in_=src)
+
+        def weave(i, on_scalar):
+            word = U32 if on_scalar else I32
+            dst = o_bf[i][:].rearrange("p c t -> p (c t)").bitcast(word).rearrange("p (c a) -> p c a", a=2)
+            src = pairs[i][:].rearrange("p a c t -> p a (c t)").bitcast(word).rearrange("p a c -> p c a")
+            if on_scalar:
+                nc.scalar.copy(out=dst, in_=src)
+            else:
+                nc.vector.tensor_copy(out=dst, in_=src)
+
         for h in range(2):
             nc.sync.dma_start(out=w_raw[h][:], in_=w_rows[:, 2 * h : 2 * h + 2, :])
-        load_set(first)
+        nc.sync.dma_start(offsets[:], slot)
+        load_set(0)
         for q in range(QUADRANTS):
             nc.scalar.dma_start(
                 out=x_scale[32 * q : 32 * q + 4, :].bitcast(I32),
                 in_=x_scales[0, 4 * q : 4 * q + 4, :].bitcast(I32),
             )
-        nc.sync.dma_start(out=x_codes[:].bitcast(I32), in_=x_words[0].rearrange("p c r -> p (c r)").bitcast(I32))
-        load_set(last)
-        load_set(second)
-
-        look_up(third, whole)
+        for h in range(2):
+            cols = slice(h * HALF, (h + 1) * HALF)
+            nc.sync.dma_start(out=x_codes[:, cols].bitcast(I32), in_=x_rows[:, cols])
+        for t in range(1, PACK):
+            load_set(t)
 
         for h in range(2):
             for u in range(2):
                 dst = w_bf[u][:].rearrange("p i m j -> p m j i")[:, :, 2 * h : 2 * h + 2, :]
-                src = w_raw[h][:].rearrange("p j (m i u) -> p m j i u", i=2, u=2)[:, :, :, :, u]
+                src = w_raw[h][:].rearrange("p j (m u i) -> p m j u i", i=2, u=2)[:, :, :, u, :]
                 split = W_ON_VECTOR if u == 0 else 0
                 if split:
                     nc.vector.tensor_copy(out=dst[:, :split], in_=src[:, :split])
-                nc.scalar.copy(out=dst[:, split:], in_=src[:, split:])
+                nc.scalar.activation(dst[:, split:], src[:, split:], ACT.Copy)
         for u in range(2):
             cols = slice(2 * u * P, (2 * u + 2) * P)
             nc.vector.quantize_mx(
@@ -155,57 +141,54 @@ def tile_picked_widxput_max_lo_kernel(tc, x_words, x_scales, mem, w1, slot, out_
                 scales=w_scale[:, cols],
                 in_=w_bf[u][:].rearrange("p i m j -> p (i m j)"),
             )
+        for t in range(PACK):
+            for h in range(2):
+                product(t, h)
 
-        look_up(first, whole)
-        for h, cols in enumerate(halves):
-            product(first, y_first[h][:], cols)
-        for t in (third, last, second):
-            product(t, y[t][:], whole[0])
+        look_up(0, 0)
+        look_up(0, 1, on_scalar=True)
+        for h in range(2):
+            larger(0, h)
+        for h in range(2):
+            put(0, h, on_scalar=True)
+        leave(0)
+        for h in range(2):
+            look_up(1, h)
+        for h in range(2):
+            larger(1, h)
+        for h in range(2):
+            put(1, h, on_scalar=True)
+        leave(1)
+        for h in range(2):
+            look_up(2, h)
+        larger(2, 0)
+        put(2, 0, on_scalar=False)
+        for h in range(2):
+            look_up(3, h)
+        for h in range(2):
+            larger(3, h)
+        larger(2, 1, tag="old3_0")
+        put(2, 1, on_scalar=False)
+        leave(2)
+        for h in range(2):
+            put(3, h, on_scalar=True)
+        leave(3)
 
-        new[first] = per_entry("new%d" % first)
-        for h, cols in enumerate(halves):
-            nc.vector.tensor_tensor(new[first][:, cols], y_first[h][:], old[first][:, cols], ALU.max)
-        look_up(last, whole)
-        for step in (compare, decide):
-            for t in (third, last):
-                step(t)
-        select(third)
-
-        o_bf = keep.tile([P, U, PACK], BF16, name="o_bf", tag="sign", align_bytes=64)
-        put(first)
-        nc.scalar.copy(out=o_bf[:, :, first], in_=store[first][:])
-
-        select(last)
-
-        look_up(second, halves)
-        larger(second, halves)
-        put(second)
-        nc.scalar.copy(out=o_bf[:, :, second], in_=store[second][:])
-        put(third)
-        nc.scalar.copy(out=o_bf[:, :, third], in_=store[third][:])
-        put(last)
-
-        parts = [slice(a, b) for a, b in zip(PARTS, PARTS[1:])]
-        for cols in parts:
-            if cols.stop <= LAST_ON_VECTOR:
-                nc.vector.tensor_copy(out=o_bf[:, cols, last], in_=store[last][:, cols])
-            else:
-                nc.scalar.copy(out=o_bf[:, cols, last], in_=store[last][:, cols])
-
-        stored = 0
-        for cols in parts:
+        for t in range(PACK):
+            for i in range(PARTS):
+                round_set(t, i)
+        for i in range(PARTS):
+            weave(i, on_scalar=i < PARTS - 1)
+        for i in (0, PARTS - 1, 1, 2):
+            cols = slice(i * PART, (i + 1) * PART)
             nc.vector.quantize_mx(
                 out=o_codes[:, cols].bitcast(FP8X4),
                 scales=o_scale[:, cols],
-                in_=o_bf[:, cols, :].rearrange("p c t -> p (c t)"),
+                in_=o_bf[i][:].rearrange("p c t -> p (c t)"),
             )
-            if cols.stop in STORE_AT[:-1]:
-                nc.sync.dma_start(out=out_words[:, stored : cols.stop], in_=o_codes[:, stored : cols.stop].bitcast(I32))
-                stored = cols.stop
-
+            nc.sync.dma_start(out=out_words[:, cols], in_=o_codes[:, cols].bitcast(I32))
         for q, queue in ((0, nc.scalar), (3, nc.sync), (2, nc.scalar), (1, nc.sync)):
             queue.dma_start(
                 out=out_2[0, 4 * q : 4 * q + 4, :].bitcast(I32),
                 in_=o_scale[32 * q : 32 * q + 4, :].bitcast(I32),
             )
-        nc.sync.dma_start(out=out_words[:, stored:], in_=o_codes[:, stored:].bitcast(I32))

@@ -19,10 +19,20 @@ P = 128
 PACK = 4
 QUADRANTS = 4
 STRIPE = 16
-HALF = T // 2
-W_ON_VECTOR = 88
-PARTS = 4
-PART = U // PARTS
+SMALL = slice(0, T // 4)
+LARGE = slice(T // 4, T)
+WHOLE = slice(0, T)
+HALVES = (slice(0, T // 2), slice(T // 2, T))
+W_ON_VECTOR = 64
+PARTS = (
+    (0, 256, False, False),
+    (256, 384, False, False),
+    (384, 640, False, True),
+    (640, 896, True, True),
+    (896, 1024, False, True),
+)
+ROUND_ORDER = (2, 0, 1, 4, 3)
+STORE_AFTER = (1, 3, 4)
 
 
 def tile_picked_widxput_max_lo_kernel(tc, x_words, x_scales, mem, w1, slot, out_0, out_1, out_2):
@@ -39,11 +49,12 @@ def tile_picked_widxput_max_lo_kernel(tc, x_words, x_scales, mem, w1, slot, out_
         w_codes = keep.tile([P, N], U32, name="w_codes", align_bytes=64)
         w_scale = keep.tile([P, N], U8, name="w_scale", align_bytes=64)
         store = [keep.tile([P, U], F32, name="store%d" % t, align_bytes=64) for t in range(PACK)]
-        pairs = [keep.tile([P, 2, PART, 2], BF16, name="pairs%d" % i, align_bytes=64) for i in range(PARTS)]
-        o_bf = [keep.tile([P, PART, PACK], BF16, name="o_bf%d" % i, align_bytes=64) for i in range(PARTS)]
+        pairs = [keep.tile([P, 2, b - a, 2], BF16, name="pairs%d" % a, align_bytes=64) for a, b, *rest in PARTS]
+        o_bf = [keep.tile([P, b - a, PACK], BF16, name="o_bf%d" % a, align_bytes=64) for a, b, *rest in PARTS]
         o_codes = keep.tile([P, U], U32, name="o_codes", align_bytes=64)
         o_scale = keep.tile([P, U], U8, name="o_scale", align_bytes=64)
-        y = {(t, h): psum.tile([P, HALF], F32, name="y%d_%d" % (t, h)) for t in range(PACK) for h in range(2)}
+        y_first = psum.tile([P, T // 4], F32, name="y_first")
+        y = [psum.tile([P, T], F32, name="y%d" % t) for t in range(PACK)]
         old, new = {}, {}
 
         w_rows = w1.rearrange("(p j) c -> p j c", j=PACK)
@@ -52,25 +63,33 @@ def tile_picked_widxput_max_lo_kernel(tc, x_words, x_scales, mem, w1, slot, out_
         x_rows = x_words[0].rearrange("p c r -> p (c r)").bitcast(I32)
         out_words = out_1[0].rearrange("p c r -> p (c r)").bitcast(I32)
 
-        def entries(h):
-            return offsets[:, h * HALF // STRIPE : (h + 1) * HALF // STRIPE]
+        def window(t, cols):
+            return store[t][:].indirect(offsets[:, cols.start // STRIPE : cols.stop // STRIPE])
+
+        def bank(t, cols):
+            return y_first[:] if (t, cols) == (0, SMALL) else y[t][:, cols]
 
         def load_set(t):
             nc.sync.dma_start(out=store[t][:], in_=mem_rows[:, t, :])
 
-        def look_up(t, h, on_scalar=False):
-            old[t, h] = keep.tile([P, HALF], F32, name="old%d_%d" % (t, h), align_bytes=64)
-            window = store[t][:].indirect(entries(h))
-            if on_scalar:
-                nc.scalar.activation(old[t, h][:], window, ACT.Copy)
-            else:
-                nc.vector.tensor_copy(old[t, h][:], window)
+        def load_x(cols):
+            nc.sync.dma_start(out=x_codes[:, cols].bitcast(I32), in_=x_rows[:, cols])
 
-        def product(t, h):
+        def move(out, in_, on_scalar):
+            if on_scalar:
+                nc.scalar.activation(out, in_, ACT.Copy)
+            else:
+                nc.vector.tensor_copy(out, in_)
+
+        def look_up(t, cols, on_scalar):
+            name = "old%d_%d" % (t, cols.start)
+            old[t, cols.start] = keep.tile([P, cols.stop - cols.start], F32, name=name, align_bytes=64)
+            move(old[t, cols.start][:], window(t, cols), on_scalar)
+
+        def product(t, cols):
             w_cols = slice(t * P, (t + 1) * P)
-            cols = slice(h * HALF, (h + 1) * HALF)
             nc.tensor.matmul_mx(
-                out=y[t, h][:],
+                out=bank(t, cols),
                 lhsT=w_codes[:, w_cols].bitcast(FP8X4),
                 lhsT_scale=w_scale[:, w_cols],
                 rhs=x_codes[:, cols].bitcast(FP8X4),
@@ -79,26 +98,26 @@ def tile_picked_widxput_max_lo_kernel(tc, x_words, x_scales, mem, w1, slot, out_
                 stop=True,
             )
 
-        def larger(t, h, tag=None):
-            name = "new%d_%d" % (t, h)
-            new[t, h] = keep.tile([P, HALF], F32, name=name, tag=tag or name, align_bytes=64)
-            nc.vector.tensor_tensor(new[t, h][:], y[t, h][:], old[t, h][:], ALU.max)
+        def larger(t, cols, out=None, tag=None):
+            if out is None:
+                name = "new%d_%d" % (t, cols.start)
+                new[t, cols.start] = keep.tile([P, cols.stop - cols.start], F32, name=name, tag=tag or name, align_bytes=64)
+                out = new[t, cols.start][:]
+            nc.vector.tensor_tensor(out, bank(t, cols), old[t, cols.start][:], ALU.max)
 
-        def put(t, h, on_scalar):
-            window = store[t][:].indirect(entries(h))
-            if on_scalar:
-                nc.scalar.activation(window, new[t, h][:], ACT.Copy)
-            else:
-                nc.vector.tensor_copy(window, new[t, h][:])
+        def put(t, cols, on_scalar):
+            move(window(t, cols), new[t, cols.start][:], on_scalar)
 
         def leave(t):
             nc.sync.dma_start(out=out_rows[:, t, :], in_=store[t][:])
 
         def round_set(t, i):
             dst = pairs[i][:, t // 2, :, t % 2]
-            src = store[t][:, i * PART : (i + 1) * PART]
+            src = store[t][:, PARTS[i][0] : PARTS[i][1]]
             if t < 2:
                 nc.gpsimd.tensor_scalar(dst, src, 1.0, 1.0, ALU.mult, ALU.mult)
+            elif PARTS[i][2]:
+                nc.scalar.copy(out=dst, in_=src)
             else:
                 nc.vector.tensor_copy(out=dst, in_=src)
 
@@ -111,18 +130,17 @@ def tile_picked_widxput_max_lo_kernel(tc, x_words, x_scales, mem, w1, slot, out_
             else:
                 nc.vector.tensor_copy(out=dst, in_=src)
 
+        nc.sync.dma_start(offsets[:], slot)
         for h in range(2):
             nc.sync.dma_start(out=w_raw[h][:], in_=w_rows[:, 2 * h : 2 * h + 2, :])
-        nc.sync.dma_start(offsets[:], slot)
+        load_x(SMALL)
         load_set(0)
         for q in range(QUADRANTS):
             nc.scalar.dma_start(
                 out=x_scale[32 * q : 32 * q + 4, :].bitcast(I32),
                 in_=x_scales[0, 4 * q : 4 * q + 4, :].bitcast(I32),
             )
-        for h in range(2):
-            cols = slice(h * HALF, (h + 1) * HALF)
-            nc.sync.dma_start(out=x_codes[:, cols].bitcast(I32), in_=x_rows[:, cols])
+        load_x(LARGE)
         for t in range(1, PACK):
             load_set(t)
 
@@ -130,10 +148,10 @@ def tile_picked_widxput_max_lo_kernel(tc, x_words, x_scales, mem, w1, slot, out_
             for u in range(2):
                 dst = w_bf[u][:].rearrange("p i m j -> p m j i")[:, :, 2 * h : 2 * h + 2, :]
                 src = w_raw[h][:].rearrange("p j (m u i) -> p m j u i", i=2, u=2)[:, :, :, u, :]
-                split = W_ON_VECTOR if u == 0 else 0
-                if split:
-                    nc.vector.tensor_copy(out=dst[:, :split], in_=src[:, :split])
-                nc.scalar.activation(dst[:, split:], src[:, split:], ACT.Copy)
+                split = W_ON_VECTOR if (h, u) == (1, 1) else P
+                nc.vector.tensor_copy(out=dst[:, :split], in_=src[:, :split])
+                if split < P:
+                    nc.scalar.activation(dst[:, split:], src[:, split:], ACT.Copy)
         for u in range(2):
             cols = slice(2 * u * P, (2 * u + 2) * P)
             nc.vector.quantize_mx(
@@ -141,54 +159,59 @@ def tile_picked_widxput_max_lo_kernel(tc, x_words, x_scales, mem, w1, slot, out_
                 scales=w_scale[:, cols],
                 in_=w_bf[u][:].rearrange("p i m j -> p (i m j)"),
             )
-        for t in range(PACK):
-            for h in range(2):
-                product(t, h)
+        for cols in (SMALL, slice(T // 4, T // 2), HALVES[1]):
+            product(0, cols)
+        for t in range(1, PACK):
+            product(t, WHOLE)
 
-        look_up(0, 0)
-        look_up(0, 1, on_scalar=True)
-        for h in range(2):
-            larger(0, h)
-        for h in range(2):
-            put(0, h, on_scalar=True)
+        look_up(0, SMALL, on_scalar=False)
+        look_up(0, LARGE, on_scalar=True)
+        larger(0, SMALL)
+        larger(0, LARGE)
+        put(0, SMALL, on_scalar=True)
+        put(0, LARGE, on_scalar=True)
         leave(0)
-        for h in range(2):
-            look_up(1, h)
-        for h in range(2):
-            larger(1, h)
-        for h in range(2):
-            put(1, h, on_scalar=True)
+        look_up(1, LARGE, on_scalar=False)
+        look_up(1, SMALL, on_scalar=False)
+        larger(1, LARGE)
+        look_up(2, SMALL, on_scalar=False)
+        put(1, LARGE, on_scalar=True)
+        look_up(2, LARGE, on_scalar=False)
+        larger(2, SMALL)
+        put(2, SMALL, on_scalar=True)
+        new[3, 0] = keep.tile([P, T], F32, name="new3", align_bytes=64)
+        for cols in HALVES:
+            look_up(3, cols, on_scalar=False)
+        for cols in HALVES:
+            larger(3, cols, out=new[3, 0][:, cols])
+        larger(1, SMALL, tag="old3_0")
+        put(1, SMALL, on_scalar=True)
         leave(1)
-        for h in range(2):
-            look_up(2, h)
-        larger(2, 0)
-        put(2, 0, on_scalar=False)
-        for h in range(2):
-            look_up(3, h)
-        for h in range(2):
-            larger(3, h)
-        larger(2, 1, tag="old3_0")
-        put(2, 1, on_scalar=False)
-        leave(2)
-        for h in range(2):
-            put(3, h, on_scalar=True)
+        larger(2, LARGE, tag="old3_256")
+        put(3, WHOLE, on_scalar=False)
         leave(3)
+        put(2, LARGE, on_scalar=True)
+        leave(2)
 
-        for t in range(PACK):
-            for i in range(PARTS):
+        for t in (0, 1, 3, 2):
+            for i in ROUND_ORDER:
                 round_set(t, i)
-        for i in range(PARTS):
-            weave(i, on_scalar=i < PARTS - 1)
-        for i in (0, PARTS - 1, 1, 2):
-            cols = slice(i * PART, (i + 1) * PART)
+        for i, part in enumerate(PARTS):
+            weave(i, on_scalar=part[3])
+        stored = 0
+        for i, part in enumerate(PARTS):
+            cols = slice(part[0], part[1])
             nc.vector.quantize_mx(
                 out=o_codes[:, cols].bitcast(FP8X4),
                 scales=o_scale[:, cols],
                 in_=o_bf[i][:].rearrange("p c t -> p (c t)"),
             )
-            nc.sync.dma_start(out=out_words[:, cols], in_=o_codes[:, cols].bitcast(I32))
+            if i in STORE_AFTER[:-1]:
+                nc.sync.dma_start(out=out_words[:, stored : cols.stop], in_=o_codes[:, stored : cols.stop].bitcast(I32))
+                stored = cols.stop
         for q, queue in ((0, nc.scalar), (3, nc.sync), (2, nc.scalar), (1, nc.sync)):
             queue.dma_start(
                 out=out_2[0, 4 * q : 4 * q + 4, :].bitcast(I32),
                 in_=o_scale[32 * q : 32 * q + 4, :].bitcast(I32),
             )
+        nc.sync.dma_start(out=out_words[:, stored:], in_=o_codes[:, stored:].bitcast(I32))

@@ -31,7 +31,7 @@ PARTS = (
     (640, 896, True, True),
     (896, 1024, False, True),
 )
-ROUND_ORDER = (2, 0, 1, 4, 3)
+UNIT = 64
 STORE_AFTER = (1, 3, 4)
 
 
@@ -49,7 +49,7 @@ def tile_picked_widxput_max_lo_kernel(tc, x_words, x_scales, mem, w1, slot, out_
         w_codes = keep.tile([P, N], U32, name="w_codes", align_bytes=64)
         w_scale = keep.tile([P, N], U8, name="w_scale", align_bytes=64)
         store = [keep.tile([P, U], F32, name="store%d" % t, align_bytes=64) for t in range(PACK)]
-        pairs = [keep.tile([P, 2, b - a, 2], BF16, name="pairs%d" % a, align_bytes=64) for a, b, *rest in PARTS]
+        pairs = keep.tile([P, U // UNIT, 2, UNIT, 2], BF16, name="pairs", align_bytes=64)
         o_bf = [keep.tile([P, b - a, PACK], BF16, name="o_bf%d" % a, align_bytes=64) for a, b, *rest in PARTS]
         o_codes = keep.tile([P, U], U32, name="o_codes", align_bytes=64)
         o_scale = keep.tile([P, U], U8, name="o_scale", align_bytes=64)
@@ -111,35 +111,37 @@ def tile_picked_widxput_max_lo_kernel(tc, x_words, x_scales, mem, w1, slot, out_
         def leave(t):
             nc.sync.dma_start(out=out_rows[:, t, :], in_=store[t][:])
 
-        def round_set(t, i):
-            dst = pairs[i][:, t // 2, :, t % 2]
-            src = store[t][:, PARTS[i][0] : PARTS[i][1]]
-            if t < 2:
+        def round_set(t, first, end, engine):
+            dst = pairs[:, first // UNIT : end // UNIT, t // 2, :, t % 2]
+            src = store[t][:, first:end].rearrange("p (n c) -> p n c", c=UNIT)
+            if engine is nc.gpsimd:
                 nc.gpsimd.tensor_scalar(dst, src, 1.0, 1.0, ALU.mult, ALU.mult)
-            elif PARTS[i][2]:
+            elif engine is nc.scalar:
                 nc.scalar.copy(out=dst, in_=src)
             else:
                 nc.vector.tensor_copy(out=dst, in_=src)
 
         def weave(i, on_scalar):
             word = U32 if on_scalar else I32
-            dst = o_bf[i][:].rearrange("p c t -> p (c t)").bitcast(word).rearrange("p (c a) -> p c a", a=2)
-            src = pairs[i][:].rearrange("p a c t -> p a (c t)").bitcast(word).rearrange("p a c -> p c a")
+            first, end = PARTS[i][:2]
+            dst = o_bf[i][:].rearrange("p c t -> p (c t)").bitcast(word).rearrange("p (n c a) -> p n c a", c=UNIT, a=2)
+            src = pairs[:, first // UNIT : end // UNIT].rearrange("p n a c t -> p n a (c t)").bitcast(word)
+            src = src.rearrange("p n a c -> p n c a")
             if on_scalar:
                 nc.scalar.copy(out=dst, in_=src)
             else:
                 nc.vector.tensor_copy(out=dst, in_=src)
 
-        nc.sync.dma_start(offsets[:], slot)
-        for h in range(2):
-            nc.sync.dma_start(out=w_raw[h][:], in_=w_rows[:, 2 * h : 2 * h + 2, :])
-        load_x(SMALL)
-        load_set(0)
         for q in range(QUADRANTS):
             nc.scalar.dma_start(
                 out=x_scale[32 * q : 32 * q + 4, :].bitcast(I32),
                 in_=x_scales[0, 4 * q : 4 * q + 4, :].bitcast(I32),
             )
+        for h in range(2):
+            nc.sync.dma_start(out=w_raw[h][:], in_=w_rows[:, 2 * h : 2 * h + 2, :])
+        load_x(SMALL)
+        load_set(0)
+        nc.sync.dma_start(offsets[:], slot)
         load_x(LARGE)
         for t in range(1, PACK):
             load_set(t)
@@ -193,9 +195,14 @@ def tile_picked_widxput_max_lo_kernel(tc, x_words, x_scales, mem, w1, slot, out_
         put(2, LARGE, on_scalar=True)
         leave(2)
 
-        for t in (0, 1, 3, 2):
-            for i in ROUND_ORDER:
-                round_set(t, i)
+        for t in (0, 1):
+            round_set(t, 0, U, nc.gpsimd)
+        round_set(3, 0, 640, nc.vector)
+        round_set(3, 896, U, nc.vector)
+        round_set(3, 640, 896, nc.scalar)
+        for first, end in ((384, 640), (0, 384), (896, U)):
+            round_set(2, first, end, nc.vector)
+        round_set(2, 640, 896, nc.scalar)
         for i, part in enumerate(PARTS):
             weave(i, on_scalar=part[3])
         stored = 0

@@ -26,10 +26,10 @@ HALVES = (slice(0, T // 2), slice(T // 2, T))
 W_ON_VECTOR = 64
 PARTS = (
     (0, 256, False, False),
-    (256, 384, False, False),
-    (384, 640, False, True),
-    (640, 896, True, True),
-    (896, 1024, False, True),
+    (256, 512, True, False),
+    (512, 768, False, True),
+    (768, 896, False, True),
+    (896, 1024, True, True),
 )
 UNIT = 64
 STORE_AFTER = (1, 3, 4)
@@ -197,12 +197,11 @@ def tile_picked_widxput_max_lo_kernel(tc, x_words, x_scales, mem, w1, slot, out_
 
         for t in (0, 1):
             round_set(t, 0, U, nc.gpsimd)
-        round_set(3, 0, 640, nc.vector)
-        round_set(3, 896, U, nc.vector)
-        round_set(3, 640, 896, nc.scalar)
-        for first, end in ((384, 640), (0, 384), (896, U)):
-            round_set(2, first, end, nc.vector)
-        round_set(2, 640, 896, nc.scalar)
+        for t in (3, 2):
+            for first, end in ((0, 256), (512, 896)):
+                round_set(t, first, end, nc.vector)
+            for first, end in ((256, 512), (896, U)):
+                round_set(t, first, end, nc.scalar)
         for i, part in enumerate(PARTS):
             weave(i, on_scalar=part[3])
         stored = 0

@@ -31,7 +31,6 @@ PARTS = (
     (768, 896, False, True),
     (896, 1024, True, True),
 )
-UNIT = 64
 STORE_AFTER = (1, 3, 4)
 
 
@@ -49,7 +48,7 @@ def tile_picked_widxput_max_lo_kernel(tc, x_words, x_scales, mem, w1, slot, out_
         w_codes = keep.tile([P, N], U32, name="w_codes", align_bytes=64)
         w_scale = keep.tile([P, N], U8, name="w_scale", align_bytes=64)
         store = [keep.tile([P, U], F32, name="store%d" % t, align_bytes=64) for t in range(PACK)]
-        pairs = keep.tile([P, U // UNIT, 2, UNIT, 2], BF16, name="pairs", align_bytes=64)
+        pairs = keep.tile([P, 2, U, 2], BF16, name="pairs", align_bytes=64)
         o_bf = [keep.tile([P, b - a, PACK], BF16, name="o_bf%d" % a, align_bytes=64) for a, b, *rest in PARTS]
         o_codes = keep.tile([P, U], U32, name="o_codes", align_bytes=64)
         o_scale = keep.tile([P, U], U8, name="o_scale", align_bytes=64)
@@ -112,8 +111,8 @@ def tile_picked_widxput_max_lo_kernel(tc, x_words, x_scales, mem, w1, slot, out_
             nc.sync.dma_start(out=out_rows[:, t, :], in_=store[t][:])
 
         def round_set(t, first, end, engine):
-            dst = pairs[:, first // UNIT : end // UNIT, t // 2, :, t % 2]
-            src = store[t][:, first:end].rearrange("p (n c) -> p n c", c=UNIT)
+            dst = pairs[:, t // 2, first:end, t % 2]
+            src = store[t][:, first:end]
             if engine is nc.gpsimd:
                 nc.gpsimd.tensor_scalar(dst, src, 1.0, 1.0, ALU.mult, ALU.mult)
             elif engine is nc.scalar:
@@ -124,9 +123,8 @@ def tile_picked_widxput_max_lo_kernel(tc, x_words, x_scales, mem, w1, slot, out_
         def weave(i, on_scalar):
             word = U32 if on_scalar else I32
             first, end = PARTS[i][:2]
-            dst = o_bf[i][:].rearrange("p c t -> p (c t)").bitcast(word).rearrange("p (n c a) -> p n c a", c=UNIT, a=2)
-            src = pairs[:, first // UNIT : end // UNIT].rearrange("p n a c t -> p n a (c t)").bitcast(word)
-            src = src.rearrange("p n a c -> p n c a")
+            dst = o_bf[i][:].rearrange("p c t -> p (c t)").bitcast(word).rearrange("p (c a) -> p c a", a=2)
+            src = pairs[:].rearrange("p a c t -> p a (c t)").bitcast(word).rearrange("p a c -> p c a")[:, first:end]
             if on_scalar:
                 nc.scalar.copy(out=dst, in_=src)
             else:
@@ -173,22 +171,22 @@ def tile_picked_widxput_max_lo_kernel(tc, x_words, x_scales, mem, w1, slot, out_
         put(0, SMALL, on_scalar=True)
         put(0, LARGE, on_scalar=True)
         leave(0)
-        look_up(1, LARGE, on_scalar=False)
-        look_up(1, SMALL, on_scalar=False)
-        larger(1, LARGE)
-        look_up(2, SMALL, on_scalar=False)
-        put(1, LARGE, on_scalar=True)
-        look_up(2, LARGE, on_scalar=False)
-        larger(2, SMALL)
-        put(2, SMALL, on_scalar=True)
+        for cols in HALVES:
+            look_up(1, cols, on_scalar=False)
+        for cols in HALVES:
+            larger(1, cols)
+        put(1, HALVES[0], on_scalar=False)
+        look_up(2, WHOLE, on_scalar=True)
+        old[2, 0], old[2, LARGE.start] = old[2, 0][:, SMALL], old[2, 0][:, LARGE]
+        put(1, HALVES[1], on_scalar=True)
+        leave(1)
         new[3, 0] = keep.tile([P, T], F32, name="new3", align_bytes=64)
         for cols in HALVES:
             look_up(3, cols, on_scalar=False)
         for cols in HALVES:
             larger(3, cols, out=new[3, 0][:, cols])
-        larger(1, SMALL, tag="old3_0")
-        put(1, SMALL, on_scalar=True)
-        leave(1)
+        larger(2, SMALL, tag="old3_0")
+        put(2, SMALL, on_scalar=True)
         larger(2, LARGE, tag="old3_256")
         put(3, WHOLE, on_scalar=False)
         leave(3)

@@ -130,6 +130,7 @@ def tile_picked_widxput_max_lo_kernel(tc, x_words, x_scales, mem, w1, slot, out_
             else:
                 nc.vector.tensor_copy(out=dst, in_=src)
 
+        nc.sync.dma_start(offsets[:], slot)
         for q in range(QUADRANTS):
             nc.scalar.dma_start(
                 out=x_scale[32 * q : 32 * q + 4, :].bitcast(I32),
@@ -139,7 +140,6 @@ def tile_picked_widxput_max_lo_kernel(tc, x_words, x_scales, mem, w1, slot, out_
             nc.sync.dma_start(out=w_raw[h][:], in_=w_rows[:, 2 * h : 2 * h + 2, :])
         load_x(SMALL)
         load_set(0)
-        nc.sync.dma_start(offsets[:], slot)
         load_x(LARGE)
         for t in range(1, PACK):
             load_set(t)

@@ -52,7 +52,7 @@ def tile_picked_widxput_max_lo_kernel(tc, x_words, x_scales, mem, w1, slot, out_
         o_bf = [keep.tile([P, b - a, PACK], BF16, name="o_bf%d" % a, align_bytes=64) for a, b, *rest in PARTS]
         o_codes = keep.tile([P, U], U32, name="o_codes", align_bytes=64)
         o_scale = keep.tile([P, U], U8, name="o_scale", align_bytes=64)
-        y_first = psum.tile([P, T // 4], F32, name="y_first")
+        y_first = [psum.tile([P, T // 4], F32, name="y_first%d" % a) for a in range(2)]
         y = [psum.tile([P, T], F32, name="y%d" % t) for t in range(PACK)]
         old, new = {}, {}
 
@@ -66,7 +66,7 @@ def tile_picked_widxput_max_lo_kernel(tc, x_words, x_scales, mem, w1, slot, out_
             return store[t][:].indirect(offsets[:, cols.start // STRIPE : cols.stop // STRIPE])
 
         def bank(t, cols):
-            return y_first[:] if (t, cols) == (0, SMALL) else y[t][:, cols]
+            return y_first[cols.start // P][:] if t == 0 and cols.stop <= T // 2 else y[t][:, cols]
 
         def load_set(t):
             nc.sync.dma_start(out=store[t][:], in_=mem_rows[:, t, :])
@@ -165,9 +165,14 @@ def tile_picked_widxput_max_lo_kernel(tc, x_words, x_scales, mem, w1, slot, out_
             product(t, WHOLE)
 
         look_up(0, SMALL, on_scalar=False)
-        look_up(0, LARGE, on_scalar=True)
+        old[0, LARGE.start] = keep.tile([P, 3 * T // 4], F32, name="old0_128", align_bytes=64)
+        move(old[0, LARGE.start][:, 64:], window(0, slice(192, T)), on_scalar=True)
+        move(old[0, LARGE.start][:, :64], window(0, slice(128, 192)), on_scalar=False)
         larger(0, SMALL)
-        larger(0, LARGE)
+        new[0, LARGE.start] = keep.tile([P, 3 * T // 4], F32, name="new0_128", align_bytes=64)
+        for cols in (slice(T // 4, T // 2), HALVES[1]):
+            within = slice(cols.start - LARGE.start, cols.stop - LARGE.start)
+            nc.vector.tensor_tensor(new[0, LARGE.start][:, within], bank(0, cols), old[0, LARGE.start][:, within], ALU.max)
         put(0, SMALL, on_scalar=True)
         put(0, LARGE, on_scalar=True)
         leave(0)

@@ -130,16 +130,16 @@ def tile_picked_widxput_max_lo_kernel(tc, x_words, x_scales, mem, w1, slot, out_
             else:
                 nc.vector.tensor_copy(out=dst, in_=src)
 
-        nc.sync.dma_start(offsets[:], slot)
         for q in range(QUADRANTS):
             nc.scalar.dma_start(
                 out=x_scale[32 * q : 32 * q + 4, :].bitcast(I32),
                 in_=x_scales[0, 4 * q : 4 * q + 4, :].bitcast(I32),
             )
-        for h in range(2):
-            nc.sync.dma_start(out=w_raw[h][:], in_=w_rows[:, 2 * h : 2 * h + 2, :])
-        load_x(SMALL)
+        nc.sync.dma_start(out=w_raw[0][:], in_=w_rows[:, 0:2, :])
+        nc.sync.dma_start(offsets[:], slot)
+        nc.sync.dma_start(out=w_raw[1][:], in_=w_rows[:, 2:4, :])
         load_set(0)
+        load_x(SMALL)
         load_x(LARGE)
         for t in range(1, PACK):
             load_set(t)

from contextlib import ExitStack

import concourse.mybir as mybir

K, T, N, U = 512, 512, 512, 1024
FLOPS = 2 * K * N * T

F32 = mybir.dt.float32
BF16 = mybir.dt.bfloat16
I32 = mybir.dt.int32
U32 = mybir.dt.uint32
U16 = mybir.dt.uint16
U8 = mybir.dt.uint8
FP8X4 = mybir.dt.float8_e4m3fn_x4
ALU = mybir.AluOpType
ACT = mybir.ActivationFunctionType

P = 128
PACK = 4
QUADRANTS = 4
STRIPE = 16
SMALL = slice(0, T // 4)
LARGE = slice(T // 4, T)
WHOLE = slice(0, T)
HALVES = (slice(0, T // 2), slice(T // 2, T))
W_ON_VECTOR = 64
PARTS = (
    (0, 256, False, False),
    (256, 512, True, False),
    (512, 768, False, True),
    (768, 896, False, True),
    (896, 1024, True, True),
)
STORE_AFTER = (1, 3, 4)


def tile_picked_widxput_max_lo_kernel(tc, x_words, x_scales, mem, w1, slot, out_0, out_1, out_2):
    nc = tc.nc
    with ExitStack() as ctx:
        keep = ctx.enter_context(tc.tile_pool(name="keep", bufs=1))
        psum = ctx.enter_context(tc.psum_pool(name="psum", bufs=1))

        offsets = keep.tile([P, T // STRIPE], U16, name="offsets")
        x_codes = keep.tile([P, T], U32, name="x_codes", align_bytes=64)
        x_scale = keep.tile([P, T], U8, name="x_scale", align_bytes=64)
        w_raw = [keep.tile([P, 2, N], F32, name="w_raw%d" % h) for h in range(2)]
        w_bf = [keep.tile([P, 2, P, PACK], BF16, name="w_bf%d" % u, align_bytes=64) for u in range(2)]
        w_codes = keep.tile([P, N], U32, name="w_codes", align_bytes=64)
        w_scale = keep.tile([P, N], U8, name="w_scale", align_bytes=64)
        store = [keep.tile([P, U], F32, name="store%d" % t, align_bytes=64) for t in range(PACK)]
        pairs = keep.tile([P, 2, U, 2], BF16, name="pairs", align_bytes=64)
        o_bf = [keep.tile([P, b - a, PACK], BF16, name="o_bf%d" % a, align_bytes=64) for a, b, *rest in PARTS]
        o_codes = keep.tile([P, U], U32, name="o_codes", align_bytes=64)
        o_scale = keep.tile([P, U], U8, name="o_scale", align_bytes=64)
        y_first = [psum.tile([P, T // 4], F32, name="y_first%d" % a) for a in range(2)]
        y = [psum.tile([P, T], F32, name="y%d" % t) for t in range(PACK)]
        old, new = {}, {}

        w_rows = w1.rearrange("(p j) c -> p j c", j=PACK)
        mem_rows = mem.rearrange("(p t) u -> p t u", t=PACK)
        out_rows = out_0.rearrange("(p t) u -> p t u", t=PACK)
        x_rows = x_words[0].rearrange("p c r -> p (c r)").bitcast(I32)
        out_words = out_1[0].rearrange("p c r -> p (c r)").bitcast(I32)

        def window(t, cols):
            return store[t][:].indirect(offsets[:, cols.start // STRIPE : cols.stop // STRIPE])

        def bank(t, cols):
            return y_first[cols.start // P][:] if t == 0 and cols.stop <= T // 2 else y[t][:, cols]

        def load_set(t):
            nc.sync.dma_start(out=store[t][:], in_=mem_rows[:, t, :])

        def load_x(cols):
            nc.sync.dma_start(out=x_codes[:, cols].bitcast(I32), in_=x_rows[:, cols])

        def move(out, in_, on_scalar):
            if on_scalar:
                nc.scalar.activation(out, in_, ACT.Copy)
            else:
                nc.vector.tensor_copy(out, in_)

        def look_up(t, cols, on_scalar):
            name = "old%d_%d" % (t, cols.start)
            old[t, cols.start] = keep.tile([P, cols.stop - cols.start], F32, name=name, align_bytes=64)
            move(old[t, cols.start][:], window(t, cols), on_scalar)

        def product(t, cols):
            w_cols = slice(t * P, (t + 1) * P)
            nc.tensor.matmul_mx(
                out=bank(t, cols),
                lhsT=w_codes[:, w_cols].bitcast(FP8X4),
                lhsT_scale=w_scale[:, w_cols],
                rhs=x_codes[:, cols].bitcast(FP8X4),
                rhs_scale=x_scale[:, cols],
                start=True,
                stop=True,
            )

        def larger(t, cols, out=None, tag=None):
            if out is None:
                name = "new%d_%d" % (t, cols.start)
                new[t, cols.start] = keep.tile([P, cols.stop - cols.start], F32, name=name, tag=tag or name, align_bytes=64)
                out = new[t, cols.start][:]
            nc.vector.tensor_tensor(out, bank(t, cols), old[t, cols.start][:], ALU.max)

        def put(t, cols, on_scalar):
            move(window(t, cols), new[t, cols.start][:], on_scalar)

        def leave(t):
            nc.sync.dma_start(out=out_rows[:, t, :], in_=store[t][:])

        def round_set(t, first, end, engine):
            dst = pairs[:, t // 2, first:end, t % 2]
            src = store[t][:, first:end]
            if engine is nc.gpsimd:
                nc.gpsimd.tensor_scalar(dst, src, 1.0, 1.0, ALU.mult, ALU.mult)
            elif engine is nc.scalar:
                nc.scalar.copy(out=dst, in_=src)
            else:
                nc.vector.tensor_copy(out=dst, in_=src)

        def weave(i, on_scalar):
            word = U32 if on_scalar else I32
            first, end = PARTS[i][:2]
            dst = o_bf[i][:].rearrange("p c t -> p (c t)").bitcast(word).rearrange("p (c a) -> p c a", a=2)
            src = pairs[:].rearrange("p a c t -> p a (c t)").bitcast(word).rearrange("p a c -> p c a")[:, first:end]
            if on_scalar:
                nc.scalar.copy(out=dst, in_=src)
            else:
                nc.vector.tensor_copy(out=dst, in_=src)

        for q in range(QUADRANTS):
            nc.scalar.dma_start(
                out=x_scale[32 * q : 32 * q + 4, :].bitcast(I32),
                in_=x_scales[0, 4 * q : 4 * q + 4, :].bitcast(I32),
            )
        nc.sync.dma_start(out=w_raw[0][:], in_=w_rows[:, 0:2, :])
        nc.sync.dma_start(offsets[:], slot)
        nc.sync.dma_start(out=w_raw[1][:], in_=w_rows[:, 2:4, :])
        load_set(0)
        load_x(SMALL)
        load_x(LARGE)
        for t in range(1, PACK):
            load_set(t)

        for h in range(2):
            for u in range(2):
                dst = w_bf[u][:].rearrange("p i m j -> p m j i")[:, :, 2 * h : 2 * h + 2, :]
                src = w_raw[h][:].rearrange("p j (m u i) -> p m j u i", i=2, u=2)[:, :, :, u, :]
                split = W_ON_VECTOR if (h, u) == (1, 1) else P
                nc.vector.tensor_copy(out=dst[:, :split], in_=src[:, :split])
                if split < P:
                    nc.scalar.activation(dst[:, split:], src[:, split:], ACT.Copy)
        for u in range(2):
            cols = slice(2 * u * P, (2 * u + 2) * P)
            nc.vector.quantize_mx(
                out=w_codes[:, cols].bitcast(FP8X4),
                scales=w_scale[:, cols],
                in_=w_bf[u][:].rearrange("p i m j -> p (i m j)"),
            )
        for cols in (SMALL, slice(T // 4, T // 2), HALVES[1]):
            product(0, cols)
        for t in range(1, PACK):
            product(t, WHOLE)

        look_up(0, SMALL, on_scalar=False)
        old[0, LARGE.start] = keep.tile([P, 3 * T // 4], F32, name="old0_128", align_bytes=64)
        move(old[0, LARGE.start][:, 64:], window(0, slice(192, T)), on_scalar=True)
        move(old[0, LARGE.start][:, :64], window(0, slice(128, 192)), on_scalar=False)
        larger(0, SMALL)
        new[0, LARGE.start] = keep.tile([P, 3 * T // 4], F32, name="new0_128", align_bytes=64)
        for cols in (slice(T // 4, T // 2), HALVES[1]):
            within = slice(cols.start - LARGE.start, cols.stop - LARGE.start)
            nc.vector.tensor_tensor(new[0, LARGE.start][:, within], bank(0, cols), old[0, LARGE.start][:, within], ALU.max)
        put(0, SMALL, on_scalar=True)
        put(0, LARGE, on_scalar=True)
        leave(0)
        for cols in HALVES:
            look_up(1, cols, on_scalar=False)
        for cols in HALVES:
            larger(1, cols)
        put(1, HALVES[0], on_scalar=False)
        look_up(2, WHOLE, on_scalar=True)
        old[2, 0], old[2, LARGE.start] = old[2, 0][:, SMALL], old[2, 0][:, LARGE]
        put(1, HALVES[1], on_scalar=True)
        leave(1)
        new[3, 0] = keep.tile([P, T], F32, name="new3", align_bytes=64)
        for cols in HALVES:
            look_up(3, cols, on_scalar=False)
        for cols in HALVES:
            larger(3, cols, out=new[3, 0][:, cols])
        larger(2, SMALL, tag="old3_0")
        put(2, SMALL, on_scalar=True)
        larger(2, LARGE, tag="old3_256")
        put(3, WHOLE, on_scalar=False)
        leave(3)
        put(2, LARGE, on_scalar=True)
        leave(2)

        for t in (0, 1):
            round_set(t, 0, U, nc.gpsimd)
        for t in (3, 2):
            for first, end in ((0, 256), (512, 896)):
                round_set(t, first, end, nc.vector)
            for first, end in ((256, 512), (896, U)):
                round_set(t, first, end, nc.scalar)
        for i, part in enumerate(PARTS):
            weave(i, on_scalar=part[3])
        stored = 0
        for i, part in enumerate(PARTS):
            cols = slice(part[0], part[1])
            nc.vector.quantize_mx(
                out=o_codes[:, cols].bitcast(FP8X4),
                scales=o_scale[:, cols],
                in_=o_bf[i][:].rearrange("p c t -> p (c t)"),
            )
            if i in STORE_AFTER[:-1]:
                nc.sync.dma_start(out=out_words[:, stored : cols.stop], in_=o_codes[:, stored : cols.stop].bitcast(I32))
                stored = cols.stop
        for q, queue in ((0, nc.scalar), (3, nc.sync), (2, nc.scalar), (1, nc.sync)):
            queue.dma_start(
                out=out_2[0, 4 * q : 4 * q + 4, :].bitcast(I32),
                in_=o_scale[32 * q : 32 * q + 4, :].bitcast(I32),
            )
        nc.sync.dma_start(out=out_words[:, stored:], in_=o_codes[:, stored:].bitcast(I32))
